import numpy as np, ml_dtypes
CORES = [242,247,114,119]
N = 4
BF = ml_dtypes.bfloat16
def gentries(a):
    return np.ascontiguousarray(a.reshape(8, 16, -1).transpose(0, 2, 1)).reshape(8, -1)
def gtable(e):
    e = np.asarray(e); return np.ascontiguousarray(e.reshape(8, -1, 16).transpose(0, 2, 1)).reshape(128, -1).astype(np.int32)
S, Q, STEPS = 2304, 128, 2
def whole(rng, *shape):
    return rng.integers(-7, 8, shape).astype(np.float32).astype(BF)
def neighbours(rng, nb):
    own = np.arange(S); nb = np.where(rng.random((N, 8, 1, S)) < 0.0625, own, nb); nb[:, :, 0] = own
    return nb.reshape(N, 128, S).astype(np.int32)
def lists(e):
    return np.stack([gtable(x) for x in e])
def setup_inputs(rng):
    return {"k": whole(rng, N, 128, S), "nb": neighbours(rng, rng.integers(0, S, (N, 8, 16, S))), "br": rng.integers(0, S, (N, 8, S)).astype(np.int32),
            "q": whole(rng, N, 128, Q), "entry": lists(rng.integers(0, S, (N, 8, Q)))}
def setup_inputs_ties(rng):
    d = setup_inputs(rng); q = np.zeros((N, 8, 16, Q), np.float32)
    for i in range(2): np.put_along_axis(q, rng.integers(0, 16, (N, 8, 1, Q)), rng.choice(np.array([-1, 1], np.float32), (N, 8, 1, Q)), 2)
    q[:, :, :, 3] = 0; d["q"] = q.reshape(N, 128, Q).astype(BF)
    nb = d["nb"].reshape(N, 8, 16, S).copy(); nb[:, :, 9:] = np.where(rng.random((N, 8, 1, S)) < 0.25, nb[:, :, 1:8], nb[:, :, 9:])
    d["nb"] = nb.reshape(N, 128, S); return d
def setup_inputs_ends(rng):
    d = setup_inputs(rng); z = np.array([0, 1, S - 2, S - 1])
    nb = d["nb"].reshape(N, 8, 16, S); nb = np.where(rng.random(nb.shape) < 0.5, z[rng.integers(0, 4, nb.shape)], nb); nb[:, :, 0] = np.arange(S); nb[:, :, :, S - 2] = S - 2
    br = d["br"]; d["br"] = np.where(rng.random(br.shape) < 0.5, z[rng.integers(0, 4, br.shape)], br).astype(np.int32)
    e = z[rng.integers(0, 4, (N, 8, Q))]; e[:, :, 0] = S - 1; e[:, :, 1] = S - 2; d["entry"] = lists(e)
    q = d["q"].astype(np.float32).reshape(N, 8, 16, Q); q[:, :, :, :2] = 7 * rng.choice(np.array([-1, 1], np.float32), (N, 8, 16, 2))
    k = d["k"].astype(np.float32).reshape(N, 8, 16, S); k[:, :, :, S - 1] = q[:, :, :, 0]; k[:, :, :, S - 2] = -q[:, :, :, 1]
    d["nb"] = nb.reshape(N, 128, S).astype(np.int32); d["q"] = q.reshape(N, 128, Q).astype(BF); d["k"] = k.reshape(N, 128, S).astype(BF); return d
def setup_inputs_one(rng):
    d = setup_inputs(rng); e = rng.integers(0, S, (N, 8, 1)); b = rng.integers(0, S, (N, 8, 1))
    d["entry"] = lists(np.repeat(e, Q, axis=2)); d["br"] = np.repeat(b, S, axis=2).astype(np.int32); return d
def setup_inputs_spread(rng):
    d = setup_inputs(rng)
    for a in ("k", "q"):
        z = rng.choice(np.array([0, 1, 2, 3, 5, 7, 7, 7]), (N, 8, 1, d[a].shape[-1])); d[a] = rng.integers(-z, z + 1, (N, 8, 16, d[a].shape[-1])).reshape(d[a].shape).astype(np.float32).astype(BF)
    low = lambda *shape: np.minimum(np.floor(S * rng.random(shape) ** 4), S - 1).astype(np.int64)
    nb = neighbours(rng, low(N, 8, 16, S)).reshape(N, 8, 16, S); nb[:, :, 2:] = np.where(rng.random((N, 8, 1, S)) < 0.25, nb[:, :, 1:2], nb[:, :, 2:])
    d["nb"] = nb.reshape(N, 128, S); d["br"] = low(N, 8, S).astype(np.int32); d["entry"] = lists(low(N, 8, Q)); return d
def check_inputs(d):
    bad = []
    for a in ("k", "q"):
        x = d[a].astype(np.float32)
        if not ((np.abs(x) <= 7) & (np.rint(x) == x)).all(): bad.append(a + "_whole")
    for a in ("nb", "br", "entry"):
        if not ((d[a] >= 0) & (d[a] < S)).all(): bad.append(a + "_range")
    if not (d["nb"][:, ::16] == np.arange(S)).all(): bad.append("nb_self")
    return bad
def reference(k, nb, br, q, entry):
    y = np.zeros((N, 8, 16, Q), np.int64); gr = np.arange(8)[:, None, None, None]; ft = np.arange(16)[None, :, None, None]
    keys = k.astype(np.float32).astype(np.int32).reshape(N, 8, 16, S); vals = k.astype(np.float32).astype(np.int32).reshape(N, 8, 16, S)
    nbs = nb.reshape(N, 8, 16, S); qs = q.astype(np.float32).astype(np.int32).reshape(N, 8, 16, Q)
    for r in range(N):
        at = gentries(entry[r])
        for s in range(N):
            t = (r + s) % N
            for step in range(STEPS):
                c = np.take_along_axis(nbs[t], at[:, None], 2)
                score = np.sum(keys[t][gr, ft, c[:, None]] * qs[r][:, :, None], axis=1)
                p = np.argmax(score, axis=1)[:, None]
                at = np.take_along_axis(c, p, 1)[:, 0]; best = np.take_along_axis(score, p, 1)
            y[r] += np.maximum(best, 0) * np.take_along_axis(vals[t], at[:, None], 2)
            at = np.take_along_axis(br[t], at, 1)
    return {"y": y.reshape(N, 128, Q).astype(np.float32)}

@@ -1,0 +1,423 @@
+from concourse.bass import DstId, RemoteDMATransfer
+from concourse.mybir import AluOpType as A, ActivationFunctionType as F, AxisListType as AX
+
+N, S, Q = 4, 2304, 128
+HALF = S // 2
+GAIN = 1280.0
+SHARE = True
+NB, NS = 2, 4
+CHUNKS = [("v", 8), ("s", 24)]
+NQD = 2
+
+SCRATCH = {"brd": ("dram", [128, S // 16], "int32"), "pt": ("psum", [128, 512], "float32")}
+for _d, _bufs in (("int32", dict(nb0=S, nb1=S, brw=S, brc=S // 16, ent=8)),
+                  ("bfloat16", dict(k0=S, k1=S, qs=N * Q, qd0=8 * Q, qd1=8 * Q, bo=128, kq=Q)),
+                  ("uint16", dict(off0=8, mid=8, offb=8 * N, snd=8 * NS * N, land=8 * NS * N)),
+                  ("float16", dict(dup=256, sel=64)),
+                  ("float32", dict(val1=256, val2=64, val3=128, ta=128, tb=128, tc=64, td=64, cut=4, d0=64, rs=Q,
+                                   term=N * Q, pin=N * Q))):
+    for _k, _n in _bufs.items():
+        SCRATCH[_k] = ("sbuf", [128, _n], _d)
+for _i in range(NS):
+    for _k, _n, _d in (("c", 16 * NB, "uint16"), ("cp", 16 * NB, "float16"), ("yb", 16 + 16 * NB, "float16"),
+                       ("gk", 256 * NB, "bfloat16"), ("xs", 128, "float16"), ("r1", 32 * NB, "float32")):
+        SCRATCH["%s%d" % (_k, _i)] = ("sbuf", [128, _n], _d)
+    SCRATCH["ps%d" % _i] = ("psum", [128, 512], "float32")
+
+SEMAPHORES = (["cv", "cs", "ct", "cg", "le", "lq", "lnb", "lk", "lbr", "lbc", "lb1", "rnb", "rk", "rbr", "loc", "st"]
+              + ["qd%d" % s for s in range(N)] + ["rq%d" % s for s in range(N)] + ["rp%d" % s for s in range(1, N)]
+              + ["rm%d_%d" % (s, i) for s in range(1, N + 1) for i in range(NS)])
+
+TIMES = [dict(cy=1.04, ga=1.62, pe=0.52, lat=80.0, hop=2600.0, issue=500.0, load=7000.0, copy=12500.0),
+         dict(cy=1.04, ga=1.25, pe=0.52, lat=120.0, hop=3500.0, issue=700.0, load=6000.0, copy=13000.0),
+         dict(cy=1.2, ga=2.2, pe=0.9, lat=60.0, hop=2000.0, issue=300.0, load=8000.0, copy=14000.0)]
+TRIES = [(stag, look) for stag in (0.0, 200.0, 400.0, 600.0, 800.0, 1000.0, 1200.0, 1600.0, 2400.0) for look in (0.0, 35.0, 70.0)]
+
+
+def walkers(T, topo):
+    near = [[t for t in range(N) if T.cores[t] in topo.cores_of(T.cores[o])] for o in range(N)]
+    if not SHARE:
+        return [[(o + s) % N for s in range(N)] for o in range(N)], near
+    partner = [[t for t in range(N) if t not in near[o]][near[o].index(o)] for o in range(N)]
+    return [[o if (o + s) % N in near[o] else partner[o] for s in range(N)] for o in range(N)], near
+
+
+def q_engines(T, topo, r, dsts):
+    eng = {d: topo.engines(T.cores[r], T.cores[d]) for d in dsts}
+    least = min(len(e) for e in eng.values())
+    narrow = [d for d in dsts if len(eng[d]) == least]
+    wide = [d for d in dsts if len(eng[d]) > least]
+    out = {}
+    for group, pool in ((narrow, eng[narrow[0]]), (wide, [e for e in eng[wide[0]] if e not in eng[narrow[0]]] if wide else [])):
+        if group:
+            share = 1
+            while share * 2 * len(group) <= len(pool):
+                share *= 2
+            for n, d in enumerate(group):
+                out[d] = pool[n * share:(n + 1) * share]
+    return out
+
+
+def build_ops(g, T, topo, r, P):
+    ops = []
+    cur = [0]
+    V, SC, PE, SY = g.vector, g.scalar, g.tensor, g.sync
+    me = T.cores[r]
+    walk, near = walkers(T, topo)
+    owner = [[o for o in range(N) if walk[o][s] == r][0] for s in range(N)]
+    sets = sorted(set(owner), key=owner.index)
+    vcost = lambda n: max(64.0, n) * P["cy"]
+    gcost = lambda n: 55.0 + P["ga"] * n
+    engines = lambda a, b: len(topo.engines(T.cores[a], T.cores[b]))
+
+    def op(eng, fn, rd, wr, cost, bank=None, hold=None, tok=None, after=None, loc=0, behind=None):
+        ops.append(dict(eng=eng, fn=fn, rd=rd, wr=wr, cost=cost, bank=bank, hold=cost if hold is None else hold,
+                        tok=tok, after=after, loc=loc, st=cur[0], behind=behind))
+        return len(ops) - 1
+
+    def vec(fn, rd, wr, n, bank=None):
+        op("v", fn, rd, wr, vcost(n), bank=bank)
+
+    def pe(fn, rd, wr, cycles, bank):
+        op("t", fn, rd, wr, 100.0 + cycles * P["pe"], bank=bank, hold=cycles * P["pe"])
+
+    def dmas(eng, pairs, sem, rd, wr, cost, behind=None):
+        q = {"y": SY, "s": SC}[eng]
+
+        def fn():
+            for o, i in pairs:
+                q.dma_start(o, i).then_inc(T.sem[sem], 16)
+        return op(eng, fn, rd, wr, cost, hold=60.0 * len(pairs), tok=(sem, 16 * len(pairs)), behind=behind)
+
+    def send(to, frm, dst, srcs, sem, rd, wr, time, issue=None):
+        rid, pid = topo.addr(T.cores[to], me)
+        mask = topo.mask(me, T.cores[to])
+        if len(srcs) == 1:
+            fn = lambda: g.remote_dma(dst, srcs[0], T.sem[sem], T.sem.loc, pid, rid, mask)
+        else:
+            fn = lambda: g.remote_dma_fused([RemoteDMATransfer(
+                dst_ids=[DstId(rid=rid, pnc=pid)], dma_engine_mask=mask, remote_sem=T.sem[sem],
+                srcs=srcs, dsts=[dst], alu_op=1)], local_sem=T.sem.loc)
+        sent = op("g", fn, rd, [], issue or P["issue"], loc=engines(r, to))
+        op(None, None, [], wr, time, tok=(sem, engines(frm, r)), after=sent)
+        return sent
+
+    a = dmas("y", [(T.brc[:], T.br[:])], "lbc", [], ["brc"], 2000.0) if SHARE else None
+    a = dmas("y", [(T.qs[:, 0:Q], T.q[:])], "lq", [], ["q0"], 2000.0, behind=a)
+    dmas("y", [(T.nb0[:], T.nb[:])], "lnb", [], ["nb0"], P["load"] - 1000.0, behind=a)
+    a = dmas("s", [(T.ent[:], T.entry[:])], "le", [], ["ent"], 2000.0)
+    vec(lambda: V.memset(T.qd0[:], 0.0), [], ["qd0"], 512)
+    a = dmas("s", [(T.qd0[16 * j:16 * j + 16, Q * j:Q * j + Q], T.q[16 * j:16 * j + 16, :]) for j in range(8)],
+             "qd0", [], ["qd0"], 2500.0, behind=a)
+    dmas("s", [(T.k0[:], T.k[:])], "lk", [], ["k0"], P["load"] - 1100.0, behind=a)
+    op("g", lambda: g.iota(T.val1[:], [[16, 8], [0, 2], [1, 16]], 0, -1, allow_small_or_imprecise_dtypes=True), [], ["val1"], 660.0)
+    op("g", lambda: g.iota(T.val2[:], [[0, 2], [32, 2], [1, 16]], 0, -1, allow_small_or_imprecise_dtypes=True), [], ["val2"], 270.0)
+    op("g", lambda: g.iota(T.val3[:], [[16, 8], [0, 16]], 0, -1, allow_small_or_imprecise_dtypes=True), [], ["val3"], 400.0)
+    guests = lambda o: sorted(set(walk[o]) - {o})
+    slot_at = lambda d, o: sorted({x for x in range(N) if d in walk[x]}, key=lambda x: walk[x].index(d)).index(o)
+    qe = q_engines(T, topo, r, guests(r))
+
+    def send_q():
+        tr = []
+        for d in guests(r):
+            rid, pid = topo.addr(T.cores[d], me)
+            u = slot_at(d, r)
+            tr.append(RemoteDMATransfer(dst_ids=[DstId(rid=rid, pnc=pid)], dma_engine_mask=sum(1 << e for e in qe[d]),
+                                        remote_sem=T.sem["rq%d" % u], src=T.qs[:, 0:Q], dst=T.qs[:, u * Q:u * Q + Q]))
+        g.remote_dma_fused(tr, local_sem=T.sem.loc)
+    a = None
+    if SHARE:
+        mate = [t for t in near[r] if t != r][0]
+        a = send(mate, mate, T.brd[:], [T.brc[:]], "rbr", ["brc"], ["brd"], 1500.0, issue=2000.0)
+    sq = op("g", send_q, ["q0"], [], P["issue"], loc=sum(len(e) for e in qe.values()), behind=a)
+    for u in range(1, len(sets)):
+        op(None, None, [], ["q%d" % u], P["hop"], tok=("rq%d" % u, len(q_engines(T, topo, sets[u], guests(sets[u]))[r])), after=sq)
+    if SHARE:
+        send(mate, mate, T.nb1[:], [T.nb0[:]], "rnb", ["nb0"], ["nb1"], P["copy"] - P["load"])
+        send(mate, mate, T.k1[:], [T.k0[:]], "rk", ["k0"], ["k1"], P["copy"] - P["load"] - 500.0)
+
+    for i in range(NS):
+        vec(lambda i=i: V.memset(T["ps%d" % i][:, 0:128], 0.0), [], ["X%d" % i], 128, bank=i)
+        vec(lambda i=i: V.memset(T["yb%d" % i][:, 0:16], 0.0), [], ["ybz%d" % i], 16)
+    vec(lambda: V.memset(T.d0[:], GAIN), [], ["d0"], 64)
+    vec(lambda: V.memset(T.qd1[:], 0.0), [], ["qd1"], 512)
+    vec(lambda: V.memset(T.d0[:, 0:64:16], -4.0e7), ["d0"], ["d0"], 4)
+    vec(lambda: V.tensor_copy(T.off0[:], T.ent[:]), ["ent"], ["off0"], 8)
+    vec(lambda: V.tensor_scalar(T.dup[:], T.val1[:], 0.0, None, A.is_equal), ["val1"], ["dup"], 256)
+    vec(lambda: V.tensor_scalar(T.tc[:], T.val2[:], 0.0, 16 * GAIN, A.is_equal, A.mult), ["val2"], ["tc"], 64)
+    vec(lambda: V.tensor_scalar(T.td[:, 0:32], T.val2[:, 0:32], -64.0, None, A.is_equal), ["val2"], ["td0"], 32)
+    vec(lambda: V.tensor_scalar(T.td[:, 32:64], T.val2[:, 32:64], -80.0, -1.0, A.is_equal, A.mult), ["val2"], ["td1"], 32)
+    vec(lambda: V.tensor_tensor(T.sel[:], T.tc[:], T.td[:], A.add), ["tc", "td0", "td1"], ["sel"], 128)
+    vec(lambda: V.tensor_reduce(T.cut[:, 2:3], T.td[:, 0:32], AX.X, A.add), ["td0"], ["cut2"], 32)
+    vec(lambda: V.tensor_reduce(T.cut[:, 3:4], T.td[:, 32:64], AX.X, A.add), ["td1"], ["cut3"], 32)
+    vec(lambda: V.tensor_scalar(T.cut[:, 0:1], T.cut[:, 3:4], -2000.0, -2000.0, A.mult, A.add), ["cut3"], ["cut0"], 1)
+    vec(lambda: V.tensor_scalar(T.cut[:, 1:2], T.cut[:, 2:3], -2000.0, 2000.0, A.mult, A.add), ["cut2"], ["cut1"], 1)
+    vec(lambda: V.tensor_scalar(T.ta[:], T.val3[:], -15.0, None, A.is_ge), ["val3"], ["ta"], 128)
+    vec(lambda: V.tensor_scalar(T.tb[:], T.val3[:], 0.0, None, A.is_le), ["val3"], ["tb"], 128)
+    vec(lambda: V.tensor_tensor(T.bo[:], T.ta[:], T.tb[:], A.mult), ["ta", "tb"], ["bo"], 256)
+    vec(lambda: V.memset(T.brw[:], 0), [], ["brz"], S)
+    dmas("y", [(T.brw[0:128:16, :], T.br[:])], "lbr", ["brz"], ["br0"], 2500.0)
+    if SHARE:
+        dmas("y", [(T.brw[1:128:16, :], T.brd[:])], "lb1", ["brz", "brd"], ["br1"], 2500.0)
+
+    def step(w, u, i, src, srck, dst, dstk):
+        n, b0 = 16 * NB, NB * i
+        c, cp, gk, xs, r1, ps = (T["%s%d" % (x, i)] for x in ("c", "cp", "gk", "xs", "r1", "ps"))
+        qdk, nbk, kk = "qd%d" % (u % NQD), "nb%d" % w, "k%d" % w
+        qd = T[qdk]
+        k = lambda x: "%s%d" % (x, i)
+        op("v", lambda: V.tensor_copy(c[:], T[nbk][:].indirect(src)), [nbk] + srck, [k("c")], gcost(n))
+        vec(lambda: V.tensor_scalar(cp[:], c[:], float(-HALF), None, A.add), [k("c")], [k("cp")], n / 2)
+
+        def nodes():
+            last = None
+            for b in range(NB):
+                for j in range(8):
+                    last = PE.matmul(ps[64 + 32 * b:96 + 32 * b, 16 * j:16 * j + 16], T.dup[:, 32 * j:32 * j + 32],
+                                     cp[:, 16 * b:16 * b + 16], True, True)
+            return last
+        pe(nodes, [k("cp"), "dup", k("X")], [k("D")], NB * 8 * 32, i)
+        j0 = 0
+        xk = []
+        for ci, (e, m) in enumerate(CHUNKS):
+            gkey = "g%d_%d" % (i, ci)
+            o, win = gk[:, 16 * j0:16 * (j0 + m)], T[kk][:].indirect(c[:, j0:j0 + m])
+            if e == "v":
+                op("v", lambda o=o, win=win: V.tensor_copy(o, win), [kk, k("c")], [gkey], gcost(16 * m))
+            else:
+                op("s", lambda o=o, win=win: SC.activation(o, win, F.Copy), [kk, k("c")], [gkey], 15.0 + gcost(16 * m))
+
+            def scores(j0=j0, m=m):
+                last = None
+                for j in range(j0, j0 + m):
+                    b, a = j // 16, j % 16
+                    last = PE.matmul(ps[32 * b:32 * b + 16, a:128:16], gk[:, 16 * j:16 * j + 16],
+                                     qd[:, 16 * b0 + j:8 * Q:Q], True, True)
+                return last
+            xk.append("X%d_%d" % (i, ci))
+            pe(scores, [gkey, qdk, k("X")], [xk[-1]], 16 * m, i)
+            j0 += m
+        vec(lambda: V.tensor_scalar(xs[:], ps[:, 0:128], T.cut[:, 0:1], T.cut[:, 1:2], A.max, A.min),
+            xk + [k("D"), "cut0", "cut1"], [k("xs")], 128, bank=i)
+        pe(lambda: PE.matmul(ps[:, 128:192], xs[:], T.sel[:], True, True), [k("xs"), "sel"], [k("S")], 64, i)
+        vec(lambda: V.tensor_tensor_scan(r1[:], T.d0[:], ps[:, 128:192], 0.0, A.add, A.max), ["d0", k("S")], [k("r1")], 64, bank=i)
+        for b in range(NB):
+            vec(lambda b=b: V.tensor_scalar(dst[:, b0 + b:b0 + b + 1], r1[:, 16 * b + 15:16 * b + 16], r1[:, 16 * b + 47:16 * b + 48],
+                                            float(HALF), A.subtract, A.add), [k("r1")], [dstk[b]], 1)
+
+    def bridge(w, s, i, obk):
+        yb, ps, slot = T["yb%d" % i], T["ps%d" % i], 8 * (NS * s + i)
+        ob, out = T.offb[:, 8 * s + NB * i:8 * s + NB * i + NB], T.snd[:, slot:slot + NB]
+        op("v", lambda: V.tensor_scalar(yb[:, 16:16 + 16 * NB], T.brw[:].indirect(ob), float(-HALF), None, A.add),
+           ["br0", "br1"] + obk, ["yb%d" % i], gcost(16 * NB))
+
+        def turn():
+            last = None
+            for odd in (1, 0):
+                for b in range(NB):
+                    for a in range(4):
+                        col = 32 * (2 * a + odd) + w
+                        last = PE.matmul(ps[32 * a:32 * a + 16 + 16 * odd, 384 + b:385 + b], yb[:, 16 * b + 16 - 16 * odd:16 * b + 32],
+                                         T.dup[:, col:col + 1], True, True)
+            return last
+        pe(turn, ["yb%d" % i, "ybz%d" % i, "dup"], ["B%d" % i], NB * 4 * 48, i)
+        vec(lambda: V.tensor_scalar(out, ps[:, 384:384 + NB], float(HALF), None, A.add), ["B%d" % i], ["snd%d_%d" % (s, i)], NB, bank=i)
+        return out
+
+    def term(s, w, u, streams, held):
+        b0, nb = NB * streams[0], NB * len(streams)
+        n, j0 = 16 * nb, 16 * b0
+        if len(streams) == 1:
+            bank, ps = streams[0], T["ps%d" % streams[0]][:, 400:400 + n]
+        else:
+            bank, ps = "t", T.pt[:, 0:n]
+        kk = "k%d" % w
+        win = T[kk][:].indirect(T.offb[:, 8 * s + b0:8 * s + b0 + nb])
+        ob = ["offb%d_%d" % (s, b) for b in range(b0, b0 + nb)]
+        ks = lambda x: ["%s%d" % (x, i) for i in streams]
+        op("v", lambda: V.tensor_tensor(T.kq[:, j0:j0 + n], win, T.qs[:, u * Q + j0:u * Q + j0 + n], A.mult),
+           [kk, "q%d" % u] + ob, ks("kq"), gcost(n))
+        pe(lambda: PE.matmul(ps, T.bo[:], T.kq[:, j0:j0 + n], True, True), ["bo"] + ks("kq"), ks("sb"), max(64, n), bank)
+        op("s", lambda: SC.activation(T.rs[:, j0:j0 + n], ps, F.Relu), ks("sb"), ks("rs"), 65.0 + n * P["cy"], bank=bank)
+        cols = lambda buf, x: T[buf][:, x * Q + j0:x * Q + j0 + n]
+        op("v", lambda: V.tensor_tensor(cols("term", s), win, T.rs[:, j0:j0 + n], A.mult), [kk] + ob + ks("rs"),
+           ks("term%d_" % s), gcost(n))
+        parts = held + [("term", s)]
+        keys = [x for buf, t in parts for x in ks("%s%d_" % (buf, t))]
+        s1 = (s + 1) % N
+        to = walk[owner[s]][s1]
+        if to != r:
+            send(to, walk[owner[s1]][s], cols("pin", s1), [cols(buf, t) for buf, t in parts],
+                 "rp%d" % s1 if s1 else "rm%d_%d" % (N, streams[0]), keys, ks("pin%d_" % s1), P["hop"])
+        elif not s1:
+            vec(lambda: V.tensor_tensor(cols("pin", 0), cols(*parts[0]), cols(*parts[1]), A.add), keys, ks("pin0_"), 2 * n)
+        if not s1:
+            dmas("y", [(T.y[:, j0:j0 + n], cols("pin", 0))], "st", ks("pin0_"), [], 2000.0)
+
+    held, built = [], {0}
+    for s in range(N):
+        o = owner[s]
+        u, w = sets.index(o), 0 if (o + s) % N == r else 1
+        stays = s < N - 1 and walk[o][s + 1] == r
+        came = s > 0 and walk[o][s - 1] != r
+        cur[0] = 0
+        if came:
+            held = [("pin", s)]
+        if u not in built:
+            built.add(u)
+            dmas("y", [(T["qd%d" % (u % NQD)][16 * j:16 * j + 16, Q * j:Q * j + Q], T.qs[16 * j:16 * j + 16, u * Q:u * Q + Q])
+                       for j in range(8)], "qd%d" % u, ["q%d" % u], ["qd%d" % (u % NQD)], 2500.0)
+        for i in range(NS):
+            cur[0] = i
+            b0, slot = NB * i, 8 * (NS * s + i)
+            if s == 0:
+                src, srck = T.off0[:, b0:b0 + NB], "off0"
+            elif came:
+                src, srck = T.land[:, slot:slot + NB], "land%d_%d" % (s, i)
+            else:
+                src, srck = T.snd[:, slot - 8 * NS:slot - 8 * NS + NB], "snd%d_%d" % (s - 1, i)
+            midk = ["mid%d" % b for b in range(b0, b0 + NB)]
+            obk = ["offb%d_%d" % (s, b) for b in range(b0, b0 + NB)]
+            step(w, u, i, src, [srck], T.mid, midk)
+            step(w, u, i, T.mid[:, b0:b0 + NB], midk, T.offb[:, 8 * s:8 * s + 8], obk)
+            if s < N - 1:
+                out = bridge(w, s, i, obk)
+                if not stays:
+                    send(walk[o][s + 1], walk[owner[s + 1]][s], T.land[:, slot + 8 * NS:slot + 8 * NS + NB], [out],
+                         "rm%d_%d" % (s + 1, i), ["snd%d_%d" % (s, i)], ["land%d_%d" % (s + 1, i)], P["hop"])
+            else:
+                term(s, w, u, [i], held)
+        if s < N - 1:
+            term(s, w, u, list(range(NS)), held)
+            held = held + [("term", s)]
+    return ops
+
+
+def find_deps(ops):
+    writer, readers, banks = {}, {}, {}
+    for n, o in enumerate(ops):
+        d = {}
+        for k in o["rd"]:
+            if k in writer:
+                d[writer[k]] = True
+        for k in o["wr"]:
+            for m in readers.get(k, []) + ([writer[k]] if k in writer else []):
+                d.setdefault(m, False)
+        if o["bank"] is not None:
+            for e, m in banks.setdefault(o["bank"], {}).items():
+                if e != o["eng"]:
+                    d.setdefault(m, False)
+            banks[o["bank"]][o["eng"]] = n
+        for k in o["rd"]:
+            readers.setdefault(k, []).append(n)
+        for k in o["wr"]:
+            writer[k], readers[k] = n, []
+        d.pop(n, None)
+        o["deps"] = d
+        o["pre"] = list(d) + [m for m in (o["after"], o["behind"]) if m is not None]
+
+
+def ready_at(ops, m, start, lat):
+    o = ops[m]
+    return max([start[p] if p == o["behind"] or (ops[p]["eng"] == o["eng"] and not o["deps"].get(p, True) and not ops[p]["tok"])
+                else start[p] + ops[p]["cost"] + lat for p in o["pre"]], default=0.0)
+
+
+def schedule(ops, lat, stag, look):
+    n = len(ops)
+    succ = [[] for _ in ops]
+    for j in range(n):
+        for m in ops[j]["pre"]:
+            succ[m].append(j)
+    level = [0.0] * n
+    for j in range(n - 1, -1, -1):
+        level[j] = ops[j]["cost"] + lat + max([level[m] for m in succ[j]], default=0.0)
+    level = [level[j] - stag * ops[j]["st"] for j in range(n)]
+    left = [len(o["pre"]) for o in ops]
+    ready = {j: 0.0 for j in range(n) if not left[j]}
+    free, begin, order = {}, [0.0] * n, []
+    while ready:
+        start = {j: max(t, free.get(ops[j]["eng"], 0.0)) if ops[j]["eng"] else t for j, t in ready.items()}
+        j = min(start, key=lambda x: (start[x], -level[x]))
+        e = ops[j]["eng"]
+        if e:
+            j = max((x for x in start if ops[x]["eng"] == e and start[x] <= start[j] + look), key=lambda x: (level[x], -x))
+            free[e] = start[j] + ops[j]["hold"]
+        begin[j] = start[j]
+        order.append(j)
+        del ready[j]
+        for m in succ[j]:
+            left[m] -= 1
+            if not left[m]:
+                ready[m] = ready_at(ops, m, begin, lat)
+    return order
+
+
+def replay(ops, order, lat):
+    free, begin = {}, [0.0] * len(ops)
+    for j in order:
+        e = ops[j]["eng"]
+        begin[j] = max(ready_at(ops, j, begin, lat), free.get(e, 0.0))
+        if e:
+            free[e] = begin[j] + ops[j]["hold"]
+    return max(begin[j] + ops[j]["cost"] for j in order), begin
+
+
+def plan(g, T, topo, r):
+    forms = []
+    for P in TIMES:
+        forms.append(build_ops(g, T, topo, r, P))
+        find_deps(forms[-1])
+    best = None
+    for stag, look in TRIES:
+        order = schedule(forms[0], TIMES[0]["lat"], stag, look)
+        spans = [replay(ops, order, P["lat"])[0] for ops, P in zip(forms, TIMES)]
+        if best is None or sum(spans) < sum(best[0]):
+            best = (spans, order, (stag, look))
+    return forms[0], best
+
+
+def rank_program(g, core, T, topo):
+    r = T.rank_of(core)
+    if r is None:
+        return
+    ops, (spans, order, _) = plan(g, T, topo, r)
+    place = {j: n for n, j in enumerate(order)}
+    queue = {"v": g.vector, "s": g.scalar, "t": g.tensor, "g": g, "y": g.sync}
+    counter = {"v": "cv", "s": "cs", "t": "ct", "g": "cg"}
+    known = {e: {} for e in queue}
+    total, waited = {}, {}
+    for j in order:
+        o = ops[j]
+        e = o["eng"]
+        if e is None:
+            o["done"], o["clock"] = o["tok"], {}
+            total[o["tok"][0]] = o["tok"][1]
+            continue
+        for m in sorted(o["deps"], key=lambda x: -place[x]):
+            p = ops[m]
+            if p["eng"] == e and not o["deps"][m] and not p["tok"]:
+                continue
+            sem, val = p["done"]
+            if known[e].get(sem, 0) < val:
+                queue[e].wait_ge(T.sem[sem], val)
+                waited[sem] = max(waited.get(sem, 0), val)
+                known[e][sem] = val
+                for x, v in p["clock"].items():
+                    known[e][x] = max(known[e].get(x, 0), v)
+        inst = o["fn"]()
+        o["clock"] = dict(known[e])
+        if o["loc"]:
+            total["loc"] = total.get("loc", 0) + o["loc"]
+            o["done"] = None
+        elif o["tok"]:
+            total[o["tok"][0]] = total.get(o["tok"][0], 0) + o["tok"][1]
+            o["done"] = (o["tok"][0], total[o["tok"][0]])
+        else:
+            sem = counter[e]
+            inst.then_inc(T.sem[sem], 1)
+            total[sem] = total.get(sem, 0) + 1
+            o["done"] = (sem, total[sem])
+    for sem, val in total.items():
+        if waited.get(sem, 0) < val:
+            (g.sync if sem == "st" else g).wait_ge(T.sem[sem], val)

@@ -3,93 +3,82 @@ from concourse.mybir import AluOpType as A, ActivationFunctionType as F, AxisLis
 
 N, S, Q = 4, 2304, 128
 HALF = S // 2
-GAIN = 1280.0
-SHARE = True
-NB, NS = 2, 4
-CHUNKS = [("v", 8), ("s", 24)]
-NQD = 2
+BIG, GAIN = 20336.0, 1168.0
+WID = [2, 2, 2, 2]
+DIRECT = False
+CHUNKS = {4: [("s", 32), ("v", 10), ("v", 10), ("s", 12)], 3: [("s", 26), ("v", 10), ("s", 12)], 2: [("s", 26), ("v", 6)]}
+SENDS = [[0], [1], [2], [3]]
+LAST = [[0, 1], [2, 3]]
+FOLD = True
+AT = dict(const=-280, c=-640, cp=220, nodes=560, s=180, v=680, xs=1510, turn=1620, scan=1640, fin=2180, yb=2460, bt=2720, snd=3100,
+          kq=2700, sb=3000, rs=3460, term=3600, add=3900, acc=1000, blocks=-1420, step=2640, bridge=880, cross=2540, late=2000,
+          old=220, look=40)
+NS = len(WID)
+EVEN = all(w % 2 == 0 for w in WID)
+B0 = [sum(WID[:i]) for i in range(NS)]
+POS = B0 if EVEN else [4 * i for i in range(NS)]
 
-SCRATCH = {"brd": ("dram", [128, S // 16], "int32"), "pt": ("psum", [128, 512], "float32")}
-for _d, _bufs in (("int32", dict(nb0=S, nb1=S, brw=S, brc=S // 16, ent=8)),
-                  ("bfloat16", dict(k0=S, k1=S, qs=N * Q, qd0=8 * Q, qd1=8 * Q, bo=128, kq=Q)),
-                  ("uint16", dict(off0=8, mid=8, offb=8 * N, snd=8 * NS * N, land=8 * NS * N)),
-                  ("float16", dict(dup=256, sel=64)),
-                  ("float32", dict(val1=256, val2=64, val3=128, ta=128, tb=128, tc=64, td=64, cut=4, d0=64, rs=Q,
-                                   term=N * Q, pin=N * Q))):
+SCRATCH = {"pb": ("psum", [128, 512], "float32"), "pt": ("psum", [128, 512], "float32")}
+for _d, _bufs in (("int32", dict(nb0=S + S // 16, nb1=S + S // 16, brw=S, ent=8)),
+                  ("bfloat16", dict(k0=S, k1=S, qs=2 * Q, qd0=8 * Q, qd1=8 * Q, bo=128, kq=Q)),
+                  ("uint16", dict(off0=16, mid=16, offb=16 * N, snd=16 * N, land=16 * N)),
+                  ("float16", dict(idn=16, sn=128, ss=128, cr=128, one=128, dup=256)),
+                  ("float32", dict(val1=256, val2=128, val3=128, val4=128, val5=16, ta=128, tb=128, e1=128, e2=128, e3=128, sg=128,
+                                   col=4, mg=8, d0=128, rs=Q, term=N * Q, pin=N * Q, acc=Q, fin=Q))):
     for _k, _n in _bufs.items():
         SCRATCH[_k] = ("sbuf", [128, _n], _d)
-for _i in range(NS):
-    for _k, _n, _d in (("c", 16 * NB, "uint16"), ("cp", 16 * NB, "float16"), ("yb", 16 + 16 * NB, "float16"),
-                       ("gk", 256 * NB, "bfloat16"), ("xs", 128, "float16"), ("r1", 32 * NB, "float32")):
-        SCRATCH["%s%d" % (_k, _i)] = ("sbuf", [128, _n], _d)
-    SCRATCH["ps%d" % _i] = ("psum", [128, 512], "float32")
+for _i, _w in enumerate(WID):
+    for _k, _n, _d in (("c", [16 * _w], "uint16"), ("cp", [_w, 32] if DIRECT else [16 * _w], "float16"), ("yb", [16 + 16 * _w], "float16"),
+                       ("gk", [256 * _w], "bfloat16"), ("xs", [128], "float16"), ("r1", [32 * _w], "float32")):
+        SCRATCH["%s%d" % (_k, _i)] = ("sbuf", [128] + _n, _d)
+    SCRATCH["px%d" % _i] = ("psum", [128, 512], "float32")
+    if DIRECT:
+        SCRATCH["pv%d" % _i] = ("psum", [128, 512], "float32")
 
-SEMAPHORES = (["cv", "cs", "ct", "cg", "le", "lq", "lnb", "lk", "lbr", "lbc", "lb1", "rnb", "rk", "rbr", "loc", "st"]
-              + ["qd%d" % s for s in range(N)] + ["rq%d" % s for s in range(N)] + ["rp%d" % s for s in range(1, N)]
-              + ["rm%d_%d" % (s, i) for s in range(1, N + 1) for i in range(NS)])
+SEMAPHORES = (["cv", "cs", "ct", "cg", "le", "lq", "lnb", "lk", "lbr", "lbc", "lb1", "rnb", "rk", "rq", "loc", "st"]
+              + ["rp%d" % s for s in range(1, N)] + ["rm%d_%d" % (s, i) for s in range(1, N + 1) for i in range(NS)])
 
-TIMES = [dict(cy=1.04, ga=1.62, pe=0.52, lat=80.0, hop=2600.0, issue=500.0, load=7000.0, copy=12500.0),
-         dict(cy=1.04, ga=1.25, pe=0.52, lat=120.0, hop=3500.0, issue=700.0, load=6000.0, copy=13000.0),
-         dict(cy=1.2, ga=2.2, pe=0.9, lat=60.0, hop=2000.0, issue=300.0, load=8000.0, copy=14000.0)]
-TRIES = [(stag, look) for stag in (0.0, 200.0, 400.0, 600.0, 800.0, 1000.0, 1200.0, 1600.0, 2400.0) for look in (0.0, 35.0, 70.0)]
+TIMES = dict(cy=0.9, ga=1.4, pe=0.46, pefix=100.0, lat=165.0, hop=2000.0, issue=600.0, load=5500.0, copy=10000.0)
 
 
 def walkers(T, topo):
     near = [[t for t in range(N) if T.cores[t] in topo.cores_of(T.cores[o])] for o in range(N)]
-    if not SHARE:
-        return [[(o + s) % N for s in range(N)] for o in range(N)], near
     partner = [[t for t in range(N) if t not in near[o]][near[o].index(o)] for o in range(N)]
-    return [[o if (o + s) % N in near[o] else partner[o] for s in range(N)] for o in range(N)], near
-
-
-def q_engines(T, topo, r, dsts):
-    eng = {d: topo.engines(T.cores[r], T.cores[d]) for d in dsts}
-    least = min(len(e) for e in eng.values())
-    narrow = [d for d in dsts if len(eng[d]) == least]
-    wide = [d for d in dsts if len(eng[d]) > least]
-    out = {}
-    for group, pool in ((narrow, eng[narrow[0]]), (wide, [e for e in eng[wide[0]] if e not in eng[narrow[0]]] if wide else [])):
-        if group:
-            share = 1
-            while share * 2 * len(group) <= len(pool):
-                share *= 2
-            for n, d in enumerate(group):
-                out[d] = pool[n * share:(n + 1) * share]
-    return out
+    return [[o if (o + s) % N in near[o] else partner[o] for s in range(N)] for o in range(N)], near, partner
 
 
 def build_ops(g, T, topo, r, P):
     ops = []
-    cur = [0]
+    now = [-1.0e5]
     V, SC, PE, SY = g.vector, g.scalar, g.tensor, g.sync
     me = T.cores[r]
-    walk, near = walkers(T, topo)
+    walk, near, partner = walkers(T, topo)
     owner = [[o for o in range(N) if walk[o][s] == r][0] for s in range(N)]
-    sets = sorted(set(owner), key=owner.index)
+    mate = [t for t in near[r] if t != r][0]
     vcost = lambda n: max(64.0, n) * P["cy"]
-    gcost = lambda n: 55.0 + P["ga"] * n
+    gcost = lambda n: 60.0 * P["cy"] + P["ga"] * n
     engines = lambda a, b: len(topo.engines(T.cores[a], T.cores[b]))
 
-    def op(eng, fn, rd, wr, cost, bank=None, hold=None, tok=None, after=None, loc=0, behind=None):
+    def op(eng, fn, rd, wr, cost, at=0.0, bank=None, hold=None, tok=None, after=None, loc=0, behind=None):
         ops.append(dict(eng=eng, fn=fn, rd=rd, wr=wr, cost=cost, bank=bank, hold=cost if hold is None else hold,
-                        tok=tok, after=after, loc=loc, st=cur[0], behind=behind))
+                        tok=tok, after=after, loc=loc, at=now[0] + at + 0.001 * len(ops), behind=behind))
         return len(ops) - 1
 
-    def vec(fn, rd, wr, n, bank=None):
-        op("v", fn, rd, wr, vcost(n), bank=bank)
+    def vec(fn, rd, wr, n, at=0.0, bank=None):
+        op("v", fn, rd, wr, vcost(n), at, bank=bank)
 
-    def pe(fn, rd, wr, cycles, bank):
-        op("t", fn, rd, wr, 100.0 + cycles * P["pe"], bank=bank, hold=cycles * P["pe"])
+    def pe(fn, rd, wr, cycles, at, bank):
+        op("t", fn, rd, wr, P["pefix"] + cycles * P["pe"], at, bank=bank, hold=cycles * P["pe"])
 
-    def dmas(eng, pairs, sem, rd, wr, cost, behind=None):
+    def dmas(eng, pairs, sem, rd, wr, cost, at=0.0, behind=None):
         q = {"y": SY, "s": SC}[eng]
 
         def fn():
             for o, i in pairs:
                 q.dma_start(o, i).then_inc(T.sem[sem], 16)
-        return op(eng, fn, rd, wr, cost, hold=60.0 * len(pairs), tok=(sem, 16 * len(pairs)), behind=behind)
+        return op(eng, fn, rd, wr, cost, at, hold=60.0 * len(pairs), tok=(sem, 16 * len(pairs)), behind=behind)
 
-    def send(to, frm, dst, srcs, sem, rd, wr, time, issue=None):
+    def send(to, dst, srcs, sem, rd, wr, time, at=0.0, issue=None, behind=None):
         rid, pid = topo.addr(T.cores[to], me)
         mask = topo.mask(me, T.cores[to])
         if len(srcs) == 1:
@@ -98,198 +87,251 @@ def build_ops(g, T, topo, r, P):
             fn = lambda: g.remote_dma_fused([RemoteDMATransfer(
                 dst_ids=[DstId(rid=rid, pnc=pid)], dma_engine_mask=mask, remote_sem=T.sem[sem],
                 srcs=srcs, dsts=[dst], alu_op=1)], local_sem=T.sem.loc)
-        sent = op("g", fn, rd, [], issue or P["issue"], loc=engines(r, to))
-        op(None, None, [], wr, time, tok=(sem, engines(frm, r)), after=sent)
+        sent = op("g", fn, rd, [], issue or P["issue"], at, loc=engines(r, to), behind=behind)
+        op(None, None, [], wr, time, tok=(sem, engines(to, r)), after=sent)
         return sent
 
-    a = dmas("y", [(T.brc[:], T.br[:])], "lbc", [], ["brc"], 2000.0) if SHARE else None
-    a = dmas("y", [(T.qs[:, 0:Q], T.q[:])], "lq", [], ["q0"], 2000.0, behind=a)
-    dmas("y", [(T.nb0[:], T.nb[:])], "lnb", [], ["nb0"], P["load"] - 1000.0, behind=a)
-    a = dmas("s", [(T.ent[:], T.entry[:])], "le", [], ["ent"], 2000.0)
-    vec(lambda: V.memset(T.qd0[:], 0.0), [], ["qd0"], 512)
-    a = dmas("s", [(T.qd0[16 * j:16 * j + 16, Q * j:Q * j + Q], T.q[16 * j:16 * j + 16, :]) for j in range(8)],
-             "qd0", [], ["qd0"], 2500.0, behind=a)
-    dmas("s", [(T.k0[:], T.k[:])], "lk", [], ["k0"], P["load"] - 1100.0, behind=a)
-    op("g", lambda: g.iota(T.val1[:], [[16, 8], [0, 2], [1, 16]], 0, -1, allow_small_or_imprecise_dtypes=True), [], ["val1"], 660.0)
-    op("g", lambda: g.iota(T.val2[:], [[0, 2], [32, 2], [1, 16]], 0, -1, allow_small_or_imprecise_dtypes=True), [], ["val2"], 270.0)
-    op("g", lambda: g.iota(T.val3[:], [[16, 8], [0, 16]], 0, -1, allow_small_or_imprecise_dtypes=True), [], ["val3"], 400.0)
-    guests = lambda o: sorted(set(walk[o]) - {o})
-    slot_at = lambda d, o: sorted({x for x in range(N) if d in walk[x]}, key=lambda x: walk[x].index(d)).index(o)
-    qe = q_engines(T, topo, r, guests(r))
-
-    def send_q():
-        tr = []
-        for d in guests(r):
-            rid, pid = topo.addr(T.cores[d], me)
-            u = slot_at(d, r)
-            tr.append(RemoteDMATransfer(dst_ids=[DstId(rid=rid, pnc=pid)], dma_engine_mask=sum(1 << e for e in qe[d]),
-                                        remote_sem=T.sem["rq%d" % u], src=T.qs[:, 0:Q], dst=T.qs[:, u * Q:u * Q + Q]))
-        g.remote_dma_fused(tr, local_sem=T.sem.loc)
+    a = dmas("y", [(T.qs[:, 0:Q], T.q[:])], "lq", [], ["q0"], 1800.0)
+    a = dmas("y", [(T.nb0[:, 0:S], T.nb[:])], "lnb", [], ["nb0"], P["load"] - 1200.0, behind=a)
+    lk = dmas("y", [(T.k0[:], T.k[:])], "lk", [], ["k0"], P["load"], behind=a)
+    a = dmas("s", [(T.ent[:], T.entry[:])], "le", [], ["ent"], 1800.0)
+    dmas("s", [(T.nb0[:, S:], T.br[:])], "lbc", [], ["brc"], 1800.0, behind=a)
+    if DIRECT:
+        counts = (("val1", 128, [[32, 4], [0, 2], [1, 16]], 0, -1), ("val3", 128, [[16, 8], [0, 16]], 0, -1),
+                  ("val2", 128, [[0, 8], [-2, 16]], 15, 0), ("val4", 128, [[0, 4], [-2, 2], [0, 16]], 1, 0),
+                  ("val5", 16, [[16, 8], [1, 2]], 0, -1))
+    else:
+        counts = (("val3", 128, [[16, 8], [0, 16]], 0, -1), ("val1", 256, [[16, 8], [0, 2], [1, 16]], 0, -1),
+                  ("val2", 64, [[32, 2], [0, 2], [1, 16]], 0, -1), ("val5", 16, [[16, 8], [1, 2]], 0, -1))
     a = None
-    if SHARE:
-        mate = [t for t in near[r] if t != r][0]
-        a = send(mate, mate, T.brd[:], [T.brc[:]], "rbr", ["brc"], ["brd"], 1500.0, issue=2000.0)
-    sq = op("g", send_q, ["q0"], [], P["issue"], loc=sum(len(e) for e in qe.values()), behind=a)
-    for u in range(1, len(sets)):
-        op(None, None, [], ["q%d" % u], P["hop"], tok=("rq%d" % u, len(q_engines(T, topo, sets[u], guests(sets[u]))[r])), after=sq)
-    if SHARE:
-        send(mate, mate, T.nb1[:], [T.nb0[:]], "rnb", ["nb0"], ["nb1"], P["copy"] - P["load"])
-        send(mate, mate, T.k1[:], [T.k0[:]], "rk", ["k0"], ["k1"], P["copy"] - P["load"] - 500.0)
+    for name, n, pattern, base, cm in counts:
+        a = op("g", lambda name=name, n=n, pattern=pattern, base=base, cm=cm:
+               g.iota(T[name][:, 0:n], pattern, base, cm, allow_small_or_imprecise_dtypes=True), [], [name], 130.0 + 1.8 * n, behind=a)
+    a = send(partner[r], T.qs[:, Q:2 * Q], [T.qs[:, 0:Q]], "rq", ["q0"], ["q1"], 4000.0, issue=2500.0, behind=a)
+    a = send(mate, T.nb1[:], [T.nb0[:]], "rnb", ["nb0", "brc"], ["nb1"], P["copy"] - P["load"], behind=a)
+    send(mate, T.k1[:], [T.k0[:]], "rk", ["k0"], ["k1"], P["copy"] - P["load"] - 500.0, behind=a)
 
-    for i in range(NS):
-        vec(lambda i=i: V.memset(T["ps%d" % i][:, 0:128], 0.0), [], ["X%d" % i], 128, bank=i)
-        vec(lambda i=i: V.memset(T["yb%d" % i][:, 0:16], 0.0), [], ["ybz%d" % i], 16)
-    vec(lambda: V.memset(T.d0[:], GAIN), [], ["d0"], 64)
-    vec(lambda: V.memset(T.qd1[:], 0.0), [], ["qd1"], 512)
-    vec(lambda: V.memset(T.d0[:, 0:64:16], -4.0e7), ["d0"], ["d0"], 4)
-    vec(lambda: V.tensor_copy(T.off0[:], T.ent[:]), ["ent"], ["off0"], 8)
-    vec(lambda: V.tensor_scalar(T.dup[:], T.val1[:], 0.0, None, A.is_equal), ["val1"], ["dup"], 256)
-    vec(lambda: V.tensor_scalar(T.tc[:], T.val2[:], 0.0, 16 * GAIN, A.is_equal, A.mult), ["val2"], ["tc"], 64)
-    vec(lambda: V.tensor_scalar(T.td[:, 0:32], T.val2[:, 0:32], -64.0, None, A.is_equal), ["val2"], ["td0"], 32)
-    vec(lambda: V.tensor_scalar(T.td[:, 32:64], T.val2[:, 32:64], -80.0, -1.0, A.is_equal, A.mult), ["val2"], ["td1"], 32)
-    vec(lambda: V.tensor_tensor(T.sel[:], T.tc[:], T.td[:], A.add), ["tc", "td0", "td1"], ["sel"], 128)
-    vec(lambda: V.tensor_reduce(T.cut[:, 2:3], T.td[:, 0:32], AX.X, A.add), ["td0"], ["cut2"], 32)
-    vec(lambda: V.tensor_reduce(T.cut[:, 3:4], T.td[:, 32:64], AX.X, A.add), ["td1"], ["cut3"], 32)
-    vec(lambda: V.tensor_scalar(T.cut[:, 0:1], T.cut[:, 3:4], -2000.0, -2000.0, A.mult, A.add), ["cut3"], ["cut0"], 1)
-    vec(lambda: V.tensor_scalar(T.cut[:, 1:2], T.cut[:, 2:3], -2000.0, 2000.0, A.mult, A.add), ["cut2"], ["cut1"], 1)
+    vec(lambda: V.memset(T.brw[:], 0), [], ["brz"], S)
     vec(lambda: V.tensor_scalar(T.ta[:], T.val3[:], -15.0, None, A.is_ge), ["val3"], ["ta"], 128)
     vec(lambda: V.tensor_scalar(T.tb[:], T.val3[:], 0.0, None, A.is_le), ["val3"], ["tb"], 128)
+    for i in range(NS):
+        op("s", lambda i=i: SC.activation(T["px%d" % i][:, 0:128], T.val3[:], F.Copy, scale=0.0), ["val3"], ["X%d" % i], vcost(128),
+           bank="x%d" % i)
+        vec(lambda i=i: V.memset(T["yb%d" % i][:, 0:16], 0.0), [], ["ybz%d" % i], 16)
+    vec(lambda: V.tensor_tensor(T.mg[:], T.ta[:, 0:128:16], T.tb[:, 0:128:16], A.mult), ["ta", "tb"], ["mg"], 16)
     vec(lambda: V.tensor_tensor(T.bo[:], T.ta[:], T.tb[:], A.mult), ["ta", "tb"], ["bo"], 256)
-    vec(lambda: V.memset(T.brw[:], 0), [], ["brz"], S)
-    dmas("y", [(T.brw[0:128:16, :], T.br[:])], "lbr", ["brz"], ["br0"], 2500.0)
-    if SHARE:
-        dmas("y", [(T.brw[1:128:16, :], T.brd[:])], "lb1", ["brz", "brd"], ["br1"], 2500.0)
+    for i in range(NS) if not EVEN else [None]:
+        a, b, n = (0, 0, 8) if EVEN else (POS[i], B0[i], WID[i])
+        vec(lambda a=a, b=b, n=n: V.tensor_copy(T.off0[:, a:a + n], T.ent[:, b:b + n]), ["ent"],
+            ["off0_%d" % x for x in (range(NS) if EVEN else [i])], 8)
+    vec(lambda: V.memset(T.d0[:], 0.0 if DIRECT else 1280.0), [], ["d0"], 128)
+    vec(lambda: V.tensor_scalar(T.idn[:], T.val5[:], 0.0, None, A.is_equal), ["val5"], ["idn"], 16)
+    vec(lambda: V.memset(T.d0[:, 0:128:16], -4.0e7), ["d0"], ["d0"], 8)
+    if DIRECT:
+        vec(lambda: V.memset(T.one[:], 1.0), [], ["one"], 64)
+        vec(lambda: V.tensor_scalar(T.e1[:], T.val1[:, 0:128], 0.0, None, A.is_equal), ["val1"], ["e1"], 128)
+        vec(lambda: V.tensor_scalar(T.e2[:], T.val1[:, 0:128], -16.0, None, A.is_equal), ["val1"], ["e2"], 128)
+        vec(lambda: V.tensor_scalar(T.sg[:], T.val4[:], 0.25, None, A.mult), ["val4"], ["sg"], 128)
+        vec(lambda: V.tensor_scalar(T.col[:, 2:3], T.val1[:, 0:1], 0.0, GAIN / 2, A.is_equal, A.mult), ["val1"], ["col2"], 1)
+        vec(lambda: V.tensor_scalar(T.col[:, 3:4], T.val1[:, 0:1], -1.0, 0.5, A.is_equal, A.mult), ["val1"], ["col3"], 1)
+        vec(lambda: V.tensor_scalar(T.ss[:], T.e1[:], BIG, None, A.mult), ["e1"], ["ss"], 128)
+        vec(lambda: V.tensor_tensor(T.e3[:], T.e1[:], T.e2[:], A.add), ["e1", "e2"], ["e3"], 256)
+        vec(lambda: V.tensor_reduce(T.col[:, 0:1], T.e1[:], AX.X, A.add), ["e1"], ["col0"], 128)
+        vec(lambda: V.tensor_reduce(T.col[:, 1:2], T.e2[:], AX.X, A.add), ["e2"], ["col1"], 128)
+        vec(lambda: V.tensor_scalar(T.cr[:], T.val2[:], T.col[:, 2:3], T.col[:, 3:4], A.mult, A.add), ["val2", "col2", "col3"], ["cr"], 128)
+        vec(lambda: V.tensor_tensor(T.sn[:], T.e3[:], T.sg[:], A.mult), ["e3", "sg"], ["sn"], 256)
+    else:
+        vec(lambda: V.tensor_scalar(T.dup[:], T.val1[:], 0.0, None, A.is_equal), ["val1"], ["dup"], 256)
+        vec(lambda: V.tensor_scalar(T.e1[:, 0:64], T.val2[:, 0:64], 0.0, 16 * 1280.0, A.is_equal, A.mult), ["val2"], ["e1"], 64)
+        for b in range(2):
+            vec(lambda b=b: V.tensor_scalar(T.e2[:, 32 * b:32 * b + 16], T.val2[:, 32 * b:32 * b + 16], -64.0, None, A.is_equal),
+                ["val2"], ["e2_%d" % b], 16)
+            vec(lambda b=b: V.tensor_scalar(T.e2[:, 32 * b + 16:32 * b + 32], T.val2[:, 32 * b + 16:32 * b + 32], -80.0, -1.0,
+                                            A.is_equal, A.mult), ["val2"], ["e3_%d" % b], 16)
+        both = ["e2_0", "e2_1", "e3_0", "e3_1"]
+        vec(lambda: V.tensor_tensor(T.ss[:, 0:64], T.e1[:, 0:64], T.e2[:, 0:64], A.add), ["e1"] + both, ["ss"], 128)
+        vec(lambda: V.tensor_reduce(T.col[:, 2:3], T.e2[:, 0:64], AX.X, A.max), both, ["col2"], 64)
+        vec(lambda: V.tensor_reduce(T.col[:, 3:4], T.e2[:, 0:64], AX.X, A.min), both, ["col3"], 64)
+        vec(lambda: V.tensor_scalar(T.col[:, 0:1], T.col[:, 3:4], -2000.0, -2000.0, A.mult, A.add), ["col3"], ["col0"], 1)
+        vec(lambda: V.tensor_scalar(T.col[:, 1:2], T.col[:, 2:3], -2000.0, 2000.0, A.mult, A.add), ["col2"], ["col1"], 1)
+    dmas("y", [(T.brw[0:128:16, :], T.br[:])], "lbr", ["brz"], ["brw"], 2500.0, behind=lk)
+
+    def blocks(u, at):
+        for j in range(8):
+            op("s", lambda j=j: SC.activation(T["qd%d" % u][:, Q * j:Q * j + Q], T.qs[:, u * Q:u * Q + Q], F.Copy, scale=T.mg[:, j:j + 1]),
+               ["q%d" % u, "mg"], ["qd%d_%d" % (u, j)], vcost(Q), at)
 
     def step(w, u, i, src, srck, dst, dstk):
-        n, b0 = 16 * NB, NB * i
-        c, cp, gk, xs, r1, ps = (T["%s%d" % (x, i)] for x in ("c", "cp", "gk", "xs", "r1", "ps"))
-        qdk, nbk, kk = "qd%d" % (u % NQD), "nb%d" % w, "k%d" % w
-        qd = T[qdk]
+        nb, b0 = WID[i], B0[i]
+        n = 16 * nb
+        c, cp, gk, xs, r1, px = (T["%s%d" % (x, i)] for x in ("c", "cp", "gk", "xs", "r1", "px"))
+        qdk, nbk, kk = ["qd%d_%d" % (u, j) for j in range(8)], "nb%d" % w, "k%d" % w
+        qd = T["qd%d" % u]
         k = lambda x: "%s%d" % (x, i)
-        op("v", lambda: V.tensor_copy(c[:], T[nbk][:].indirect(src)), [nbk] + srck, [k("c")], gcost(n))
-        vec(lambda: V.tensor_scalar(cp[:], c[:], float(-HALF), None, A.add), [k("c")], [k("cp")], n / 2)
-
-        def nodes():
-            last = None
-            for b in range(NB):
-                for j in range(8):
-                    last = PE.matmul(ps[64 + 32 * b:96 + 32 * b, 16 * j:16 * j + 16], T.dup[:, 32 * j:32 * j + 32],
-                                     cp[:, 16 * b:16 * b + 16], True, True)
-            return last
-        pe(nodes, [k("cp"), "dup", k("X")], [k("D")], NB * 8 * 32, i)
-        j0 = 0
+        op("v", lambda: V.tensor_copy(c[:], T[nbk][:, 0:S].indirect(src)), [nbk] + srck, [k("c")], gcost(n), AT["c"])
         xk = []
-        for ci, (e, m) in enumerate(CHUNKS):
+        if DIRECT:
+            pv, vb = T[k("pv")][:, 0:2 * n], k("v")
+            pe(lambda: PE.matmul(pv, T.one[:], T.cr[:, 0:2 * n], True, False), ["one", "cr"], [k("V")], 2 * n, AT["const"], vb)
+            for h in range(2):
+                vec(lambda h=h: V.tensor_scalar(cp[:, :, 16 * h:16 * h + 16], c[:], float(-HALF), T.col[:, h:h + 1], A.add, A.mult),
+                    [k("c"), "col%d" % h], [k("cp%d_" % h)], n / 2, AT["cp"])
+        else:
+            pv, vb = px[:, 128:128 + 2 * n], k("x")
+            vec(lambda: V.tensor_scalar(cp[:], c[:], float(-HALF), None, A.add), [k("c")], [k("cp0_")], n / 2, AT["cp"])
+        for b in range(nb):
+            def nodes(b=b):
+                last = None
+                if DIRECT:
+                    for a in range(4):
+                        last = PE.matmul(pv[32 * a:32 * a + 32, 32 * b:32 * b + 32], cp[:, b, :], T.sn[:, 32 * a:32 * a + 32], False, False)
+                else:
+                    for j in range(8):
+                        last = PE.matmul(px[64 + 32 * b:96 + 32 * b, 16 * j:16 * j + 16], T.dup[:, 32 * j:32 * j + 32],
+                                         cp[:, 16 * b:16 * b + 16], True, True)
+                return last
+            if DIRECT:
+                pe(nodes, [k("cp0_"), k("cp1_"), "sn"], [k("V")], 128, AT["nodes"], vb)
+            else:
+                xk.append("D%d_%d" % (i, b))
+                pe(nodes, [k("cp0_"), "dup", k("X")], [xk[-1]], 256, AT["nodes"], vb)
+        j0 = 0
+        due = {"v": AT["v"], "s": AT["s"]}
+        for ci, (e, m) in enumerate(CHUNKS[nb]):
             gkey = "g%d_%d" % (i, ci)
             o, win = gk[:, 16 * j0:16 * (j0 + m)], T[kk][:].indirect(c[:, j0:j0 + m])
             if e == "v":
-                op("v", lambda o=o, win=win: V.tensor_copy(o, win), [kk, k("c")], [gkey], gcost(16 * m))
+                op("v", lambda o=o, win=win: V.tensor_copy(o, win), [kk, k("c")], [gkey], gcost(16 * m), due[e])
             else:
-                op("s", lambda o=o, win=win: SC.activation(o, win, F.Copy), [kk, k("c")], [gkey], 15.0 + gcost(16 * m))
+                op("s", lambda o=o, win=win: SC.activation(o, win, F.Copy), [kk, k("c")], [gkey], 15.0 + gcost(16 * m), due[e])
+            due[e] += gcost(16 * m)
 
             def scores(j0=j0, m=m):
                 last = None
                 for j in range(j0, j0 + m):
                     b, a = j // 16, j % 16
-                    last = PE.matmul(ps[32 * b:32 * b + 16, a:128:16], gk[:, 16 * j:16 * j + 16],
+                    last = PE.matmul(px[32 * b:32 * b + 16, a:128:16], gk[:, 16 * j:16 * j + 16],
                                      qd[:, 16 * b0 + j:8 * Q:Q], True, True)
                 return last
             xk.append("X%d_%d" % (i, ci))
-            pe(scores, [gkey, qdk, k("X")], [xk[-1]], 16 * m, i)
+            pe(scores, [gkey, k("X")] + qdk, [xk[-1]], 16 * m, due[e] + P["lat"], k("x"))
             j0 += m
-        vec(lambda: V.tensor_scalar(xs[:], ps[:, 0:128], T.cut[:, 0:1], T.cut[:, 1:2], A.max, A.min),
-            xk + [k("D"), "cut0", "cut1"], [k("xs")], 128, bank=i)
-        pe(lambda: PE.matmul(ps[:, 128:192], xs[:], T.sel[:], True, True), [k("xs"), "sel"], [k("S")], 64, i)
-        vec(lambda: V.tensor_tensor_scan(r1[:], T.d0[:], ps[:, 128:192], 0.0, A.add, A.max), ["d0", k("S")], [k("r1")], 64, bank=i)
-        for b in range(NB):
-            vec(lambda b=b: V.tensor_scalar(dst[:, b0 + b:b0 + b + 1], r1[:, 16 * b + 15:16 * b + 16], r1[:, 16 * b + 47:16 * b + 48],
-                                            float(HALF), A.subtract, A.add), [k("r1")], [dstk[b]], 1)
+        if DIRECT:
+            vec(lambda: V.tensor_copy(xs[:], px[:, 0:128]), xk, [k("xs")], 128, AT["xs"], bank=k("x"))
+        else:
+            vec(lambda: V.tensor_scalar(xs[:], px[:, 0:128], T.col[:, 0:1], T.col[:, 1:2], A.max, A.min), xk + ["col0", "col1"],
+                [k("xs")], 128, AT["xs"], bank=k("x"))
+        pe(lambda: PE.matmul(pv, xs[:], T.ss[:, 0:2 * n], not DIRECT, True), [k("xs"), "ss"], [k("V")], 2 * n, AT["turn"], vb)
+        vec(lambda: V.tensor_tensor_scan(r1[:], T.d0[:, 0:2 * n], pv, 0.0, A.add, A.max), ["d0", k("V")], [k("r1")], 2 * n,
+            AT["scan"], bank=vb)
+        for b in range(nb):
+            vec(lambda b=b: V.tensor_scalar(dst[:, b:b + 1], r1[:, 32 * b + 15:32 * b + 16], r1[:, 32 * b + 31:32 * b + 32],
+                                            float(HALF), A.subtract, A.add), [k("r1")], [dstk[b]], 1, AT["fin"])
 
     def bridge(w, s, i, obk):
-        yb, ps, slot = T["yb%d" % i], T["ps%d" % i], 8 * (NS * s + i)
-        ob, out = T.offb[:, 8 * s + NB * i:8 * s + NB * i + NB], T.snd[:, slot:slot + NB]
-        op("v", lambda: V.tensor_scalar(yb[:, 16:16 + 16 * NB], T.brw[:].indirect(ob), float(-HALF), None, A.add),
-           ["br0", "br1"] + obk, ["yb%d" % i], gcost(16 * NB))
+        nb, at = WID[i], 16 * s + POS[i]
+        yb, ps = T["yb%d" % i], T["px%d" % i][:, 384:384 + nb]
+        op("v", lambda: V.tensor_scalar(yb[:, 16:16 + 16 * nb], T.brw[:].indirect(T.offb[:, at:at + nb]), float(-HALF), None, A.add),
+           ["brw"] + obk, ["yb%d" % i], gcost(16 * nb), AT["yb"])
 
         def turn():
             last = None
             for odd in (1, 0):
-                for b in range(NB):
+                for b in range(nb):
                     for a in range(4):
-                        col = 32 * (2 * a + odd) + w
-                        last = PE.matmul(ps[32 * a:32 * a + 16 + 16 * odd, 384 + b:385 + b], yb[:, 16 * b + 16 - 16 * odd:16 * b + 32],
-                                         T.dup[:, col:col + 1], True, True)
+                        col = 2 * (2 * a + odd) + w
+                        last = PE.matmul(ps[32 * a:32 * a + 16 + 16 * odd, b:b + 1], yb[:, 16 * b + 16 - 16 * odd:16 * b + 32],
+                                         T.idn[:, col:col + 1], True, True)
             return last
-        pe(turn, ["yb%d" % i, "ybz%d" % i, "dup"], ["B%d" % i], NB * 4 * 48, i)
-        vec(lambda: V.tensor_scalar(out, ps[:, 384:384 + NB], float(HALF), None, A.add), ["B%d" % i], ["snd%d_%d" % (s, i)], NB, bank=i)
-        return out
+        pe(turn, ["yb%d" % i, "ybz%d" % i, "idn"], ["B%d" % i], nb * 4 * 48, AT["bt"], "x%d" % i)
+        vec(lambda: V.tensor_scalar(T.snd[:, at:at + nb], ps, float(HALF), None, A.add), ["B%d" % i], ["snd%d_%d" % (s, i)], nb,
+            AT["snd"], bank="x%d" % i)
 
-    def term(s, w, u, streams, held):
-        b0, nb = NB * streams[0], NB * len(streams)
-        n, j0 = 16 * nb, 16 * b0
-        if len(streams) == 1:
-            bank, ps = streams[0], T["ps%d" % streams[0]][:, 400:400 + n]
-        else:
-            bank, ps = "t", T.pt[:, 0:n]
+    def term(s, w, u, streams, bank):
+        i = streams[0]
+        nb = sum(WID[x] for x in streams)
+        n, j0, at = 16 * nb, 16 * B0[i], 16 * s + POS[i]
+        ps = T[bank][:, j0:j0 + n]
         kk = "k%d" % w
-        win = T[kk][:].indirect(T.offb[:, 8 * s + b0:8 * s + b0 + nb])
-        ob = ["offb%d_%d" % (s, b) for b in range(b0, b0 + nb)]
-        ks = lambda x: ["%s%d" % (x, i) for i in streams]
+        win = T[kk][:].indirect(T.offb[:, at:at + nb])
+        ob = ["offb%d_%d_%d" % (s, x, b) for x in streams for b in range(WID[x])]
+        ks = lambda y: ["%s%d" % (y, x) for x in streams]
+        early = AT["yb"] - AT["kq"] if s == N - 1 else 0
         op("v", lambda: V.tensor_tensor(T.kq[:, j0:j0 + n], win, T.qs[:, u * Q + j0:u * Q + j0 + n], A.mult),
-           [kk, "q%d" % u] + ob, ks("kq"), gcost(n))
-        pe(lambda: PE.matmul(ps, T.bo[:], T.kq[:, j0:j0 + n], True, True), ["bo"] + ks("kq"), ks("sb"), max(64, n), bank)
-        op("s", lambda: SC.activation(T.rs[:, j0:j0 + n], ps, F.Relu), ks("sb"), ks("rs"), 65.0 + n * P["cy"], bank=bank)
-        cols = lambda buf, x: T[buf][:, x * Q + j0:x * Q + j0 + n]
-        op("v", lambda: V.tensor_tensor(cols("term", s), win, T.rs[:, j0:j0 + n], A.mult), [kk] + ob + ks("rs"),
-           ks("term%d_" % s), gcost(n))
-        parts = held + [("term", s)]
-        keys = [x for buf, t in parts for x in ks("%s%d_" % (buf, t))]
-        s1 = (s + 1) % N
-        to = walk[owner[s]][s1]
-        if to != r:
-            send(to, walk[owner[s1]][s], cols("pin", s1), [cols(buf, t) for buf, t in parts],
-                 "rp%d" % s1 if s1 else "rm%d_%d" % (N, streams[0]), keys, ks("pin%d_" % s1), P["hop"])
-        elif not s1:
-            vec(lambda: V.tensor_tensor(cols("pin", 0), cols(*parts[0]), cols(*parts[1]), A.add), keys, ks("pin0_"), 2 * n)
-        if not s1:
-            dmas("y", [(T.y[:, j0:j0 + n], cols("pin", 0))], "st", ks("pin0_"), [], 2000.0)
+           [kk, "q%d" % u] + ob, ks("kq"), gcost(n), AT["kq"] + early)
+        pe(lambda: PE.matmul(ps, T.bo[:], T.kq[:, j0:j0 + n], True, True), ["bo"] + ks("kq"), ks("sb"), max(64, n), AT["sb"] + early, bank)
+        op("s", lambda: SC.activation(T.rs[:, j0:j0 + n], ps, F.Relu), ks("sb"), ks("rs"), vcost(n), AT["rs"] + early, bank=bank)
+        op("v", lambda: V.tensor_tensor(T.term[:, s * Q + j0:s * Q + j0 + n], win, T.rs[:, j0:j0 + n], A.mult), [kk] + ob + ks("rs"),
+           ks("term%d_" % s), gcost(n), AT["term"] + early)
 
-    held, built = [], {0}
+    every = list(range(NS))
+    part = lambda x, j0=0, n=Q: T[x[0]][:, x[1] * Q + j0:x[1] * Q + j0 + n]
+    keys = lambda parts, streams: ["%s%d_%d" % (buf, t, i) for buf, t in parts for i in streams]
+    held, waiting, base = [], [], 0.0
+    blocks(0, 0.0)
     for s in range(N):
         o = owner[s]
-        u, w = sets.index(o), 0 if (o + s) % N == r else 1
+        u, w = 0 if o == r else 1, 0 if (o + s) % N == r else 1
         stays = s < N - 1 and walk[o][s + 1] == r
         came = s > 0 and walk[o][s - 1] != r
-        cur[0] = 0
+        now[0] = base
         if came:
             held = [("pin", s)]
-        if u not in built:
-            built.add(u)
-            dmas("y", [(T["qd%d" % (u % NQD)][16 * j:16 * j + 16, Q * j:Q * j + Q], T.qs[16 * j:16 * j + 16, u * Q:u * Q + Q])
-                       for j in range(8)], "qd%d" % u, ["q%d" % u], ["qd%d" % (u % NQD)], 2500.0)
-        for i in range(NS):
-            cur[0] = i
-            b0, slot = NB * i, 8 * (NS * s + i)
+            if u and owner[s - 1] == r:
+                blocks(1, AT["blocks"])
+        if s == N - 1 and len(held) > 1 and not FOLD:
+            vec(lambda held=held: V.tensor_tensor(T.acc[:], part(held[0]), part(held[1]), A.add), keys(held, every),
+                keys([("acc", 0)], every), 2 * Q, AT["acc"])
+            held = [("acc", 0)]
+        for i in every:
+            now[0] = base + AT["step"] * B0[i] / 8
+            nb, at = WID[i], 16 * s + POS[i]
             if s == 0:
-                src, srck = T.off0[:, b0:b0 + NB], "off0"
-            elif came:
-                src, srck = T.land[:, slot:slot + NB], "land%d_%d" % (s, i)
+                src, srck = T.off0[:, at:at + nb], "off0_%d" % i
             else:
-                src, srck = T.snd[:, slot - 8 * NS:slot - 8 * NS + NB], "snd%d_%d" % (s - 1, i)
-            midk = ["mid%d" % b for b in range(b0, b0 + NB)]
-            obk = ["offb%d_%d" % (s, b) for b in range(b0, b0 + NB)]
-            step(w, u, i, src, [srck], T.mid, midk)
-            step(w, u, i, T.mid[:, b0:b0 + NB], midk, T.offb[:, 8 * s:8 * s + 8], obk)
+                src, srck = T["land" if came else "snd"][:, at - 16:at - 16 + nb], "%s%d_%d" % ("land" if came else "snd", s - 1, i)
+            mid = T.mid[:, POS[i]:POS[i] + nb]
+            midk = ["mid%d_%d" % (i, b) for b in range(nb)]
+            obk = ["offb%d_%d_%d" % (s, i, b) for b in range(nb)]
+            step(w, u, i, src, [srck], mid, midk)
+            now[0] += AT["step"]
+            step(w, u, i, mid, midk, T.offb[:, at:at + nb], obk)
             if s < N - 1:
-                out = bridge(w, s, i, obk)
-                if not stays:
-                    send(walk[o][s + 1], walk[owner[s + 1]][s], T.land[:, slot + 8 * NS:slot + 8 * NS + NB], [out],
-                         "rm%d_%d" % (s + 1, i), ["snd%d_%d" % (s, i)], ["land%d_%d" % (s + 1, i)], P["hop"])
-            else:
-                term(s, w, u, [i], held)
+                bridge(w, s, i, obk)
+                for group in SENDS:
+                    if not stays and group[-1] == i:
+                        a, b = 16 * s + POS[group[0]], at + nb
+                        send(partner[r], T.land[:, a:b], [T.snd[:, a:b]], "rm%d_%d" % (s + 1, i), keys([("snd", s)], group),
+                             keys([("land", s)], group), P["hop"], AT["snd"])
+            for group in LAST:
+                if s == N - 1 and group[-1] == i:
+                    term(s, w, u, group, ("pt", "pb")[LAST.index(group) % 2])
+                    j0, n = 16 * B0[group[0]], 16 * sum(WID[x] for x in group)
+                    both, fin, pin = held + [("term", s)], ("fin", 0), ("pin", 0)
+                    if o == r or not FOLD:
+                        vec(lambda j0=j0, n=n, both=both: V.tensor_tensor(part(fin, j0, n), part(both[0], j0, n), part(both[1], j0, n), A.add),
+                            keys(both, group), keys([fin], group), 2 * n, AT["add"] + AT["yb"] - AT["kq"])
+                        both = [fin]
+                    if o != r:
+                        send(o, part(pin, j0, n), [part(x, j0, n) for x in both], "rm%d_%d" % (N, i), keys(both, group),
+                             keys([pin], group), P["hop"], AT["add"])
+                    out = fin if o == r else pin
+                    dmas("y", [(T.y[:, j0:j0 + n], part(out, j0, n))], "st", keys([out], group), [], 2000.0, AT["add"])
+        if s == 0:
+            dmas("y", [(T.brw[1:128:16, :], T.nb1[:, S:])], "lb1", ["nb1"], ["brw"], 2500.0, AT["yb"])
         if s < N - 1:
-            term(s, w, u, list(range(NS)), held)
+            waiting.append((s, w, u))
+            if not stays or s == N - 2:
+                for n, x in enumerate(reversed(waiting)):
+                    for streams in ([every] if EVEN else [[i] for i in every]):
+                        now[0] = base + AT["step"] * (1 + B0[streams[-1]] / 8) + (AT["late"] if stays else AT["old"] * n)
+                        term(*x, streams, "pt")
+                waiting = []
             held = held + [("term", s)]
+            if not stays:
+                send(partner[r], part(("pin", s + 1)), [part(x) for x in held], "rp%d" % (s + 1), keys(held, every),
+                     keys([("pin", s + 1)], every), P["hop"], AT["add"])
+        base += 2 * AT["step"] + AT["bridge"] + (0 if stays else AT["cross"])
     return ops
 
 
@@ -323,25 +365,21 @@ def ready_at(ops, m, start, lat):
                 else start[p] + ops[p]["cost"] + lat for p in o["pre"]], default=0.0)
 
 
-def schedule(ops, lat, stag, look):
+def schedule(ops, lat, look):
     n = len(ops)
     succ = [[] for _ in ops]
     for j in range(n):
         for m in ops[j]["pre"]:
             succ[m].append(j)
-    level = [0.0] * n
-    for j in range(n - 1, -1, -1):
-        level[j] = ops[j]["cost"] + lat + max([level[m] for m in succ[j]], default=0.0)
-    level = [level[j] - stag * ops[j]["st"] for j in range(n)]
     left = [len(o["pre"]) for o in ops]
     ready = {j: 0.0 for j in range(n) if not left[j]}
     free, begin, order = {}, [0.0] * n, []
     while ready:
         start = {j: max(t, free.get(ops[j]["eng"], 0.0)) if ops[j]["eng"] else t for j, t in ready.items()}
-        j = min(start, key=lambda x: (start[x], -level[x]))
+        j = min(start, key=lambda x: (start[x], ops[x]["at"]))
         e = ops[j]["eng"]
         if e:
-            j = max((x for x in start if ops[x]["eng"] == e and start[x] <= start[j] + look), key=lambda x: (level[x], -x))
+            j = min((x for x in start if ops[x]["eng"] == e and start[x] <= start[j] + look), key=lambda x: ops[x]["at"])
             free[e] = start[j] + ops[j]["hold"]
         begin[j] = start[j]
         order.append(j)
@@ -353,35 +391,13 @@ def schedule(ops, lat, stag, look):
     return order
 
 
-def replay(ops, order, lat):
-    free, begin = {}, [0.0] * len(ops)
-    for j in order:
-        e = ops[j]["eng"]
-        begin[j] = max(ready_at(ops, j, begin, lat), free.get(e, 0.0))
-        if e:
-            free[e] = begin[j] + ops[j]["hold"]
-    return max(begin[j] + ops[j]["cost"] for j in order), begin
-
-
-def plan(g, T, topo, r):
-    forms = []
-    for P in TIMES:
-        forms.append(build_ops(g, T, topo, r, P))
-        find_deps(forms[-1])
-    best = None
-    for stag, look in TRIES:
-        order = schedule(forms[0], TIMES[0]["lat"], stag, look)
-        spans = [replay(ops, order, P["lat"])[0] for ops, P in zip(forms, TIMES)]
-        if best is None or sum(spans) < sum(best[0]):
-            best = (spans, order, (stag, look))
-    return forms[0], best
-
-
 def rank_program(g, core, T, topo):
     r = T.rank_of(core)
     if r is None:
         return
-    ops, (spans, order, _) = plan(g, T, topo, r)
+    ops = build_ops(g, T, topo, r, TIMES)
+    find_deps(ops)
+    order = schedule(ops, TIMES["lat"], AT["look"])
     place = {j: n for n, j in enumerate(order)}
     queue = {"v": g.vector, "s": g.scalar, "t": g.tensor, "g": g, "y": g.sync}
     counter = {"v": "cv", "s": "cs", "t": "ct", "g": "cg"}

@@ -1,44 +1,43 @@
+import math
 from concourse.bass import DstId, RemoteDMATransfer
 from concourse.mybir import AluOpType as A, ActivationFunctionType as F, AxisListType as AX
 
 N, S, Q = 4, 2304, 128
 HALF = S // 2
-BIG, GAIN = 20336.0, 1168.0
-WID = [2, 2, 2, 2]
-DIRECT = False
-CHUNKS = {4: [("s", 32), ("v", 10), ("v", 10), ("s", 12)], 3: [("s", 26), ("v", 10), ("s", 12)], 2: [("s", 26), ("v", 6)]}
+BIG, GAIN = 21248.0, 1200.0
+NONE = -1600.0
+NS, NB = 4, 2
+SHARE = dict(start=[14, 16, 10, 8], came=[10, 10, 12, 8], first=[2, 8, 12, 10], second=[8, 8, 8, 8], last=[6, 2, 6, 4])
+SPLIT = dict(start=0, came=6, first=0, second=0, last=0)
 SENDS = [[0], [1], [2], [3]]
-LAST = [[0, 1], [2, 3]]
-FOLD = True
-AT = dict(const=-280, c=-640, cp=220, nodes=560, s=180, v=680, xs=1510, turn=1620, scan=1640, fin=2180, yb=2460, bt=2720, snd=3100,
-          kq=2700, sb=3000, rs=3460, term=3600, add=3900, acc=1000, blocks=-1420, step=2640, bridge=880, cross=2540, late=2000,
-          old=220, look=40)
-NS = len(WID)
-EVEN = all(w % 2 == 0 for w in WID)
-B0 = [sum(WID[:i]) for i in range(NS)]
-POS = B0 if EVEN else [4 * i for i in range(NS)]
+LAST = [[0], [1], [2], [3]]
+GATE = True
+FAST = True
+OVER = [[0], [1], [2], [3]]
+FOLD = 0
+AT = dict(c=-1440, cp=140, nodes=560, s=-60, v=520, xs=1510, turn=1380, scan=2200, fin=2340, yb=2780, bt=3120, snd=3140,
+          kb=3140, kq=2740, sb=2680, rs=2980, term=3600, add=3740, acc=720, blocks=-780, step=2800, bridge=560, cross=1060,
+          late=1880, gap=0, soon=120, end=2620, look=40)
 
-SCRATCH = {"pb": ("psum", [128, 512], "float32"), "pt": ("psum", [128, 512], "float32")}
-for _d, _bufs in (("int32", dict(nb0=S + S // 16, nb1=S + S // 16, brw=S, ent=8)),
-                  ("bfloat16", dict(k0=S, k1=S, qs=2 * Q, qd0=8 * Q, qd1=8 * Q, bo=128, kq=Q)),
-                  ("uint16", dict(off0=16, mid=16, offb=16 * N, snd=16 * N, land=16 * N)),
-                  ("float16", dict(idn=16, sn=128, ss=128, cr=128, one=128, dup=256)),
-                  ("float32", dict(val1=256, val2=128, val3=128, val4=128, val5=16, ta=128, tb=128, e1=128, e2=128, e3=128, sg=128,
-                                   col=4, mg=8, d0=128, rs=Q, term=N * Q, pin=N * Q, acc=Q, fin=Q))):
+SCRATCH = {_k: ("psum", [128, 512], "float32") for _k in ("pb", "pt", "pq")}
+for _d, _bufs in (("int32", dict(nb0=S, nb1=S, brw=S, brc=S // 16, brd=S // 16, ent=8)),
+                  ("bfloat16", dict(k0=S + 16, k1=S + 16, qs=2 * Q, qd0=8 * Q, qd1=8 * Q, bo=128, kq=2 * Q, kb=2 * Q,
+                                    one=256, dup=256, sgn=68, sel=68, idn=16)),
+                  ("uint16", dict(off0=8, mid=8, offb=8 * N, snd=8 * N, land=8 * N)),
+                  ("float16", dict(yb=48 * NS)),
+                  ("float32", dict(val=8, ta=8, tb=8, mg=8, col=8, gain=68, term=N * Q, pin=N * Q, sum=Q, acc=Q, fin=Q))):
     for _k, _n in _bufs.items():
         SCRATCH[_k] = ("sbuf", [128, _n], _d)
-for _i, _w in enumerate(WID):
-    for _k, _n, _d in (("c", [16 * _w], "uint16"), ("cp", [_w, 32] if DIRECT else [16 * _w], "float16"), ("yb", [16 + 16 * _w], "float16"),
-                       ("gk", [256 * _w], "bfloat16"), ("xs", [128], "float16"), ("r1", [32 * _w], "float32")):
-        SCRATCH["%s%d" % (_k, _i)] = ("sbuf", [128] + _n, _d)
+for _i in range(NS):
+    for _k, _n, _d in (("c", 16 * NB, "uint16"), ("cp", 16 * NB, "float16"),
+                       ("gk", 256 * NB, "bfloat16"), ("xs", 128, "float16"), ("r1", 68, "float32")):
+        SCRATCH["%s%d" % (_k, _i)] = ("sbuf", [128, _n], _d)
     SCRATCH["px%d" % _i] = ("psum", [128, 512], "float32")
-    if DIRECT:
-        SCRATCH["pv%d" % _i] = ("psum", [128, 512], "float32")
 
-SEMAPHORES = (["cv", "cs", "ct", "cg", "le", "lq", "lnb", "lk", "lbr", "lbc", "lb1", "rnb", "rk", "rq", "loc", "st"]
+SEMAPHORES = (["cv", "cs", "ct", "cg", "le", "lq", "lnb", "lk", "lbr", "lbc", "lb1", "rnb", "rk", "rbr", "rq", "loc", "st"]
               + ["rp%d" % s for s in range(1, N)] + ["rm%d_%d" % (s, i) for s in range(1, N + 1) for i in range(NS)])
 
-TIMES = dict(cy=0.9, ga=1.4, pe=0.46, pefix=100.0, lat=165.0, hop=2000.0, issue=600.0, load=5500.0, copy=10000.0)
+TIMES = dict(cy=0.9, ga=1.4, pe=0.4, pefix=170.0, lat=160.0, own=145.0, hop=1500.0, issue=400.0, column=14.0, load=4500.0, copy=9000.0)
 
 
 def walkers(T, topo):
@@ -48,7 +47,7 @@ def walkers(T, topo):
 
 
 def build_ops(g, T, topo, r, P):
-    ops = []
+    ops, gathers = [], []
     now = [-1.0e5]
     V, SC, PE, SY = g.vector, g.scalar, g.tensor, g.sync
     me = T.cores[r]
@@ -70,15 +69,11 @@ def build_ops(g, T, topo, r, P):
     def pe(fn, rd, wr, cycles, at, bank):
         op("t", fn, rd, wr, P["pefix"] + cycles * P["pe"], at, bank=bank, hold=cycles * P["pe"])
 
-    def dmas(eng, pairs, sem, rd, wr, cost, at=0.0, behind=None):
+    def dma(eng, out, in_, sem, rd, wr, cost, at=0.0, behind=None):
         q = {"y": SY, "s": SC}[eng]
+        return op(eng, lambda: q.dma_start(out, in_).then_inc(T.sem[sem], 16), rd, wr, cost, at, hold=60.0, tok=(sem, 16), behind=behind)
 
-        def fn():
-            for o, i in pairs:
-                q.dma_start(o, i).then_inc(T.sem[sem], 16)
-        return op(eng, fn, rd, wr, cost, at, hold=60.0 * len(pairs), tok=(sem, 16 * len(pairs)), behind=behind)
-
-    def send(to, dst, srcs, sem, rd, wr, time, at=0.0, issue=None, behind=None):
+    def send(to, dst, srcs, sem, rd, wr, time, at=0.0, issue=None, behind=None, wide=0):
         rid, pid = topo.addr(T.cores[to], me)
         mask = topo.mask(me, T.cores[to])
         if len(srcs) == 1:
@@ -88,122 +83,100 @@ def build_ops(g, T, topo, r, P):
                 dst_ids=[DstId(rid=rid, pnc=pid)], dma_engine_mask=mask, remote_sem=T.sem[sem],
                 srcs=srcs, dsts=[dst], alu_op=1)], local_sem=T.sem.loc)
         sent = op("g", fn, rd, [], issue or P["issue"], at, loc=engines(r, to), behind=behind)
+        time += P["column"] * wide * len(srcs)
         op(None, None, [], wr, time, tok=(sem, engines(to, r)), after=sent)
         return sent
 
-    a = dmas("y", [(T.qs[:, 0:Q], T.q[:])], "lq", [], ["q0"], 1800.0)
-    a = dmas("y", [(T.nb0[:, 0:S], T.nb[:])], "lnb", [], ["nb0"], P["load"] - 1200.0, behind=a)
-    lk = dmas("y", [(T.k0[:], T.k[:])], "lk", [], ["k0"], P["load"], behind=a)
-    a = dmas("s", [(T.ent[:], T.entry[:])], "le", [], ["ent"], 1800.0)
-    dmas("s", [(T.nb0[:, S:], T.br[:])], "lbc", [], ["brc"], 1800.0, behind=a)
-    if DIRECT:
-        counts = (("val1", 128, [[32, 4], [0, 2], [1, 16]], 0, -1), ("val3", 128, [[16, 8], [0, 16]], 0, -1),
-                  ("val2", 128, [[0, 8], [-2, 16]], 15, 0), ("val4", 128, [[0, 4], [-2, 2], [0, 16]], 1, 0),
-                  ("val5", 16, [[16, 8], [1, 2]], 0, -1))
-    else:
-        counts = (("val3", 128, [[16, 8], [0, 16]], 0, -1), ("val1", 256, [[16, 8], [0, 2], [1, 16]], 0, -1),
-                  ("val2", 64, [[32, 2], [0, 2], [1, 16]], 0, -1), ("val5", 16, [[16, 8], [1, 2]], 0, -1))
-    a = None
-    for name, n, pattern, base, cm in counts:
-        a = op("g", lambda name=name, n=n, pattern=pattern, base=base, cm=cm:
-               g.iota(T[name][:, 0:n], pattern, base, cm, allow_small_or_imprecise_dtypes=True), [], [name], 130.0 + 1.8 * n, behind=a)
+    a = dma("y", T.qs[:, 0:Q], T.q[:], "lq", [], ["q0"], 1800.0)
+    a = dma("y", T.nb0[:], T.nb[:], "lnb", [], ["nb0"], P["load"] - 1200.0, behind=a)
+    a = dma("y", T.k0[:, 0:S], T.k[:], "lk", [], ["k0"], P["load"], behind=a)
+    a = dma("y", T.brc[:], T.br[:], "lbc", [], ["brc"], P["load"] + 200.0, behind=a)
+    dma("s", T.ent[:], T.entry[:], "le", [], ["ent"], 1800.0)
+    vec(lambda: V.memset(T.one[:], 1.0), [], ["one"], 128)
+    vec(lambda: V.memset(T.k0[:, S:], 0.0), [], ["kz"], 16)
+    for n in range(S // 256):
+        vec(lambda n=n: V.memset(T.brw[:, 256 * n:256 * n + 256], 0), [], ["brz%d" % n], 256, 3.0)
+    dma("y", T.brw[0:128:16, :], T.br[:], "lbr", ["brz%d" % n for n in range(S // 256)], ["brw"], 2500.0, behind=a)
+    def pick(out, in_, pattern, base, test, fill, rd, wr, behind, sign=1):
+        return op("g", lambda: g.affine_select(out, in_, [[sign * a, n] for a, n in pattern], test, fill, sign * base, -sign), rd, wr,
+                  170.0 + 1.8 * math.prod(n for a, n in pattern), behind=behind)
+
+    flag = dict(allow_small_or_imprecise_dtypes=True)
+    a = op("g", lambda: g.iota(T.val[:], [[16, 8]], 0, -1, **flag), [], ["val"], 150.0)
+    a = op("g", lambda: g.iota(T.sgn[:], [[0, NB], [-2, 2], [0, 17]], 1, 0, **flag), [], ["sgn"], 250.0, behind=a)
+    a = pick(T.dup[:], T.one[:], [[16, 8], [0, 2], [1, 16]], 0, A.is_equal, 0.0, ["one"], ["dup"], a)
+    a = pick(T.sgn[:], T.sgn[:], [[32, NB], [16, 2], [1, 17]], 64, A.is_equal, 0.0, ["sgn"], ["sgn"], a)
+    a = pick(T.sel[:], T.sgn[:], [[32, NB], [0, 2], [1, 17]], 0, A.not_equal, BIG, ["sgn"], ["sel"], a)
     a = send(partner[r], T.qs[:, Q:2 * Q], [T.qs[:, 0:Q]], "rq", ["q0"], ["q1"], 4000.0, issue=2500.0, behind=a)
-    a = send(mate, T.nb1[:], [T.nb0[:]], "rnb", ["nb0", "brc"], ["nb1"], P["copy"] - P["load"], behind=a)
-    send(mate, T.k1[:], [T.k0[:]], "rk", ["k0"], ["k1"], P["copy"] - P["load"] - 500.0, behind=a)
+    a = send(mate, T.nb1[:], [T.nb0[:]], "rnb", ["nb0"], ["nb1"], P["copy"] - P["load"], behind=a)
+    a = send(mate, T.k1[:], [T.k0[:]], "rk", ["k0", "kz"], ["k1"], P["copy"] - P["load"] - 500.0, behind=a)
+    a = send(mate, T.brd[:], [T.brc[:]], "rbr", ["brc"], ["brd"], P["copy"] - P["load"] - 500.0, behind=a)
+    a = pick(T.idn[:], T.one[:, 0:16], [[16, 8], [1, 2]], 0, A.is_equal, 0.0, ["one"], ["idn"], a)
+    a = pick(T.bo[:], T.one[:, 0:128], [[16, 8], [0, 16]], 15, A.is_ge, 0.0, ["one"], ["bo"], a)
+    pick(T.bo[:], T.bo[:], [[16, 8], [0, 16]], 0, A.is_ge, 0.0, ["bo"], ["bo"], a, -1)
 
-    vec(lambda: V.memset(T.brw[:], 0), [], ["brz"], S)
-    vec(lambda: V.tensor_scalar(T.ta[:], T.val3[:], -15.0, None, A.is_ge), ["val3"], ["ta"], 128)
-    vec(lambda: V.tensor_scalar(T.tb[:], T.val3[:], 0.0, None, A.is_le), ["val3"], ["tb"], 128)
+    col, mg = (lambda n: T.col[:, n:n + 1]), (lambda n: T.mg[:, n:n + 1])
+    vec(lambda: V.tensor_scalar(T.ta[:], T.val[:], -15.0, None, A.is_ge), ["val"], ["ta"], 8)
+    vec(lambda: V.tensor_scalar(T.tb[:], T.val[:], 0.0, None, A.is_le), ["val"], ["tb"], 8)
+    vec(lambda: V.memset(T.gain[:], GAIN), [], ["gain"], 68)
+    vec(lambda: V.tensor_tensor(T.mg[:], T.ta[:], T.tb[:], A.mult), ["ta", "tb"], ["mg"], 16)
+    vec(lambda: V.memset(T.gain[:, 0:68:17], -4.0e7), ["gain"], ["gain"], 4)
+    vec(lambda: V.memset(T.yb[:], 0.0), [], ["ybz"], 96)
+    vec(lambda: V.memset(T.gain[:, 16:68:17], 0.0), ["gain"], ["gain"], 4)
+    ends = ((1.0, (5, 7)), (-1.0, (4, 6)))
+    for n, (sign, rows) in enumerate(ends):
+        vec(lambda n=n, sign=sign: V.tensor_scalar(col(4 + n), mg(1), 1.0 + sign * 2000.0, -sign * 2000.0, A.mult, A.add), ["mg"],
+            ["col%d" % (4 + n)], 1)
+    for m in range(2):
+        for n, (sign, rows) in enumerate(ends):
+            a, b = 4 - 2 * m + n, 2 - 2 * m + n
+            vec(lambda a=a, b=b, sign=sign, row=rows[m]: V.tensor_scalar(col(b), mg(row), sign * 2000.0, col(a), A.mult, A.add),
+                ["mg", "col%d" % a], ["col%d" % b], 1)
+    for v in range(2):
+        vec(lambda v=v: V.tensor_scalar(T.sel[:, 16 + 17 * v:68:34], T.one[:, 0:2], mg(1), (NONE - HALF * v) / 16, A.mult, A.mult),
+            ["mg", "sel", "one"], ["sel%d" % v], 2)
+    vec(lambda: V.tensor_copy(T.off0[:], T.ent[:]), ["ent"], ["off0"], 8)
     for i in range(NS):
-        op("s", lambda i=i: SC.activation(T["px%d" % i][:, 0:128], T.val3[:], F.Copy, scale=0.0), ["val3"], ["X%d" % i], vcost(128),
+        op("s", lambda i=i: SC.activation(T["px%d" % i][:, 0:128], T.one[:, 0:128], F.Copy, scale=0.0), ["one"], ["X%d" % i], vcost(128),
            bank="x%d" % i)
-        vec(lambda i=i: V.memset(T["yb%d" % i][:, 0:16], 0.0), [], ["ybz%d" % i], 16)
-    vec(lambda: V.tensor_tensor(T.mg[:], T.ta[:, 0:128:16], T.tb[:, 0:128:16], A.mult), ["ta", "tb"], ["mg"], 16)
-    vec(lambda: V.tensor_tensor(T.bo[:], T.ta[:], T.tb[:], A.mult), ["ta", "tb"], ["bo"], 256)
-    for i in range(NS) if not EVEN else [None]:
-        a, b, n = (0, 0, 8) if EVEN else (POS[i], B0[i], WID[i])
-        vec(lambda a=a, b=b, n=n: V.tensor_copy(T.off0[:, a:a + n], T.ent[:, b:b + n]), ["ent"],
-            ["off0_%d" % x for x in (range(NS) if EVEN else [i])], 8)
-    vec(lambda: V.memset(T.d0[:], 0.0 if DIRECT else 1280.0), [], ["d0"], 128)
-    vec(lambda: V.tensor_scalar(T.idn[:], T.val5[:], 0.0, None, A.is_equal), ["val5"], ["idn"], 16)
-    vec(lambda: V.memset(T.d0[:, 0:128:16], -4.0e7), ["d0"], ["d0"], 8)
-    if DIRECT:
-        vec(lambda: V.memset(T.one[:], 1.0), [], ["one"], 64)
-        vec(lambda: V.tensor_scalar(T.e1[:], T.val1[:, 0:128], 0.0, None, A.is_equal), ["val1"], ["e1"], 128)
-        vec(lambda: V.tensor_scalar(T.e2[:], T.val1[:, 0:128], -16.0, None, A.is_equal), ["val1"], ["e2"], 128)
-        vec(lambda: V.tensor_scalar(T.sg[:], T.val4[:], 0.25, None, A.mult), ["val4"], ["sg"], 128)
-        vec(lambda: V.tensor_scalar(T.col[:, 2:3], T.val1[:, 0:1], 0.0, GAIN / 2, A.is_equal, A.mult), ["val1"], ["col2"], 1)
-        vec(lambda: V.tensor_scalar(T.col[:, 3:4], T.val1[:, 0:1], -1.0, 0.5, A.is_equal, A.mult), ["val1"], ["col3"], 1)
-        vec(lambda: V.tensor_scalar(T.ss[:], T.e1[:], BIG, None, A.mult), ["e1"], ["ss"], 128)
-        vec(lambda: V.tensor_tensor(T.e3[:], T.e1[:], T.e2[:], A.add), ["e1", "e2"], ["e3"], 256)
-        vec(lambda: V.tensor_reduce(T.col[:, 0:1], T.e1[:], AX.X, A.add), ["e1"], ["col0"], 128)
-        vec(lambda: V.tensor_reduce(T.col[:, 1:2], T.e2[:], AX.X, A.add), ["e2"], ["col1"], 128)
-        vec(lambda: V.tensor_scalar(T.cr[:], T.val2[:], T.col[:, 2:3], T.col[:, 3:4], A.mult, A.add), ["val2", "col2", "col3"], ["cr"], 128)
-        vec(lambda: V.tensor_tensor(T.sn[:], T.e3[:], T.sg[:], A.mult), ["e3", "sg"], ["sn"], 256)
-    else:
-        vec(lambda: V.tensor_scalar(T.dup[:], T.val1[:], 0.0, None, A.is_equal), ["val1"], ["dup"], 256)
-        vec(lambda: V.tensor_scalar(T.e1[:, 0:64], T.val2[:, 0:64], 0.0, 16 * 1280.0, A.is_equal, A.mult), ["val2"], ["e1"], 64)
-        for b in range(2):
-            vec(lambda b=b: V.tensor_scalar(T.e2[:, 32 * b:32 * b + 16], T.val2[:, 32 * b:32 * b + 16], -64.0, None, A.is_equal),
-                ["val2"], ["e2_%d" % b], 16)
-            vec(lambda b=b: V.tensor_scalar(T.e2[:, 32 * b + 16:32 * b + 32], T.val2[:, 32 * b + 16:32 * b + 32], -80.0, -1.0,
-                                            A.is_equal, A.mult), ["val2"], ["e3_%d" % b], 16)
-        both = ["e2_0", "e2_1", "e3_0", "e3_1"]
-        vec(lambda: V.tensor_tensor(T.ss[:, 0:64], T.e1[:, 0:64], T.e2[:, 0:64], A.add), ["e1"] + both, ["ss"], 128)
-        vec(lambda: V.tensor_reduce(T.col[:, 2:3], T.e2[:, 0:64], AX.X, A.max), both, ["col2"], 64)
-        vec(lambda: V.tensor_reduce(T.col[:, 3:4], T.e2[:, 0:64], AX.X, A.min), both, ["col3"], 64)
-        vec(lambda: V.tensor_scalar(T.col[:, 0:1], T.col[:, 3:4], -2000.0, -2000.0, A.mult, A.add), ["col3"], ["col0"], 1)
-        vec(lambda: V.tensor_scalar(T.col[:, 1:2], T.col[:, 2:3], -2000.0, 2000.0, A.mult, A.add), ["col2"], ["col1"], 1)
-    dmas("y", [(T.brw[0:128:16, :], T.br[:])], "lbr", ["brz"], ["brw"], 2500.0, behind=lk)
 
-    def blocks(u, at):
+    def blocks(u, at, behind=None):
         for j in range(8):
             op("s", lambda j=j: SC.activation(T["qd%d" % u][:, Q * j:Q * j + Q], T.qs[:, u * Q:u * Q + Q], F.Copy, scale=T.mg[:, j:j + 1]),
-               ["q%d" % u, "mg"], ["qd%d_%d" % (u, j)], vcost(Q), at)
+               ["q%d" % u, "mg"], ["qd%d_%d" % (u, j)], vcost(Q), at, behind=behind)
+        op("s", lambda: SC.activation(T.pq[:, u * Q:u * Q + Q], T.qs[:, u * Q:u * Q + Q], F.Copy), ["q%d" % u], ["pq%d" % u], vcost(Q),
+           at, bank="q", behind=behind)
 
-    def step(w, u, i, src, srck, dst, dstk):
-        nb, b0 = WID[i], B0[i]
-        n = 16 * nb
+    def step(kind, w, u, i, src, srck, dst, dstk):
+        n, read = 16 * NB, 16 if kind == "last" else 15
         c, cp, gk, xs, r1, px = (T["%s%d" % (x, i)] for x in ("c", "cp", "gk", "xs", "r1", "px"))
         qdk, nbk, kk = ["qd%d_%d" % (u, j) for j in range(8)], "nb%d" % w, "k%d" % w
-        qd = T["qd%d" % u]
+        qd, pv = T["qd%d" % u], px[:, 128:196]
         k = lambda x: "%s%d" % (x, i)
-        op("v", lambda: V.tensor_copy(c[:], T[nbk][:, 0:S].indirect(src)), [nbk] + srck, [k("c")], gcost(n), AT["c"])
+        op("v", lambda: V.tensor_copy(c[:], T[nbk][:].indirect(src)), [nbk] + srck, [k("c")], gcost(n), AT["c"])
+        vec(lambda: V.tensor_scalar(cp[:], c[:], float(-HALF), None, A.add), [k("c")], [k("cp")], n / 2, AT["cp"])
         xk = []
-        if DIRECT:
-            pv, vb = T[k("pv")][:, 0:2 * n], k("v")
-            pe(lambda: PE.matmul(pv, T.one[:], T.cr[:, 0:2 * n], True, False), ["one", "cr"], [k("V")], 2 * n, AT["const"], vb)
-            for h in range(2):
-                vec(lambda h=h: V.tensor_scalar(cp[:, :, 16 * h:16 * h + 16], c[:], float(-HALF), T.col[:, h:h + 1], A.add, A.mult),
-                    [k("c"), "col%d" % h], [k("cp%d_" % h)], n / 2, AT["cp"])
-        else:
-            pv, vb = px[:, 128:128 + 2 * n], k("x")
-            vec(lambda: V.tensor_scalar(cp[:], c[:], float(-HALF), None, A.add), [k("c")], [k("cp0_")], n / 2, AT["cp"])
-        for b in range(nb):
+        for b in range(NB):
             def nodes(b=b):
                 last = None
-                if DIRECT:
-                    for a in range(4):
-                        last = PE.matmul(pv[32 * a:32 * a + 32, 32 * b:32 * b + 32], cp[:, b, :], T.sn[:, 32 * a:32 * a + 32], False, False)
-                else:
-                    for j in range(8):
-                        last = PE.matmul(px[64 + 32 * b:96 + 32 * b, 16 * j:16 * j + 16], T.dup[:, 32 * j:32 * j + 32],
-                                         cp[:, 16 * b:16 * b + 16], True, True)
+                for j in range(8):
+                    last = PE.matmul(px[64 + 32 * b:96 + 32 * b, 16 * j:16 * j + 16], T.dup[:, 32 * j:32 * j + 32],
+                                     cp[:, 16 * b:16 * b + 16], True, True)
                 return last
-            if DIRECT:
-                pe(nodes, [k("cp0_"), k("cp1_"), "sn"], [k("V")], 128, AT["nodes"], vb)
-            else:
-                xk.append("D%d_%d" % (i, b))
-                pe(nodes, [k("cp0_"), "dup", k("X")], [xk[-1]], 256, AT["nodes"], vb)
+            xk.append("D%d_%d" % (i, b))
+            pe(nodes, [k("cp"), "dup", k("X")], [xk[-1]], 256, AT["nodes"], k("x"))
         j0 = 0
         due = {"v": AT["v"], "s": AT["s"]}
-        for ci, (e, m) in enumerate(CHUNKS[nb]):
+        mine, end = SHARE[kind][i], min(SPLIT[kind], max(0, n - SHARE[kind][i] - 8))
+        for ci, (e, m) in enumerate((("s", n - mine - end), ("v", mine), ("s", end))):
+            if not m:
+                continue
             gkey = "g%d_%d" % (i, ci)
-            o, win = gk[:, 16 * j0:16 * (j0 + m)], T[kk][:].indirect(c[:, j0:j0 + m])
+            o, win = gk[:, 16 * j0:16 * (j0 + m)], T[kk][:, 0:S].indirect(c[:, j0:j0 + m])
             if e == "v":
                 op("v", lambda o=o, win=win: V.tensor_copy(o, win), [kk, k("c")], [gkey], gcost(16 * m), due[e])
             else:
-                op("s", lambda o=o, win=win: SC.activation(o, win, F.Copy), [kk, k("c")], [gkey], 15.0 + gcost(16 * m), due[e])
+                gathers.append(op("s", lambda o=o, win=win: SC.activation(o, win, F.Copy), [kk, k("c")], [gkey], 15.0 + gcost(16 * m), due[e]))
             due[e] += gcost(16 * m)
 
             def scores(j0=j0, m=m):
@@ -211,63 +184,62 @@ def build_ops(g, T, topo, r, P):
                 for j in range(j0, j0 + m):
                     b, a = j // 16, j % 16
                     last = PE.matmul(px[32 * b:32 * b + 16, a:128:16], gk[:, 16 * j:16 * j + 16],
-                                     qd[:, 16 * b0 + j:8 * Q:Q], True, True)
+                                     qd[:, n * i + j:8 * Q:Q], True, True)
                 return last
             xk.append("X%d_%d" % (i, ci))
             pe(scores, [gkey, k("X")] + qdk, [xk[-1]], 16 * m, due[e] + P["lat"], k("x"))
             j0 += m
-        if DIRECT:
-            vec(lambda: V.tensor_copy(xs[:], px[:, 0:128]), xk, [k("xs")], 128, AT["xs"], bank=k("x"))
-        else:
-            vec(lambda: V.tensor_scalar(xs[:], px[:, 0:128], T.col[:, 0:1], T.col[:, 1:2], A.max, A.min), xk + ["col0", "col1"],
-                [k("xs")], 128, AT["xs"], bank=k("x"))
-        pe(lambda: PE.matmul(pv, xs[:], T.ss[:, 0:2 * n], not DIRECT, True), [k("xs"), "ss"], [k("V")], 2 * n, AT["turn"], vb)
-        vec(lambda: V.tensor_tensor_scan(r1[:], T.d0[:, 0:2 * n], pv, 0.0, A.add, A.max), ["d0", k("V")], [k("r1")], 2 * n,
-            AT["scan"], bank=vb)
-        for b in range(nb):
-            vec(lambda b=b: V.tensor_scalar(dst[:, b:b + 1], r1[:, 32 * b + 15:32 * b + 16], r1[:, 32 * b + 31:32 * b + 32],
-                                            float(HALF), A.subtract, A.add), [k("r1")], [dstk[b]], 1, AT["fin"])
+        vec(lambda: V.tensor_scalar(xs[:], px[:, 0:128], col(0), col(1), A.max, A.min), xk + ["col0", "col1"],
+            [k("xs")], 128, AT["xs"], bank=k("x"))
+        pe(lambda: PE.matmul(pv, xs[:], T.sel[:], True, True), [k("xs"), "sel0", "sel1"], [k("V")], 68, AT["turn"], k("x"))
+        vec(lambda: V.tensor_tensor_scan(r1[:], T.gain[:], pv, 0.0, A.add, A.max), ["gain", k("V")], [k("r1")], 68, AT["scan"], bank=k("x"))
+        for b in range(NB):
+            e1, e2 = 34 * b + read, 34 * b + 17 + read
+            vec(lambda b=b, e1=e1, e2=e2: V.tensor_scalar(dst[:, b:b + 1], r1[:, e1:e1 + 1], r1[:, e2:e2 + 1], float(HALF), A.subtract, A.add),
+                [k("r1")], [dstk[b]], 1, AT["fin"])
 
-    def bridge(w, s, i, obk):
-        nb, at = WID[i], 16 * s + POS[i]
-        yb, ps = T["yb%d" % i], T["px%d" % i][:, 384:384 + nb]
+    def bridge(w, s, streams):
+        i, nb = streams[-1], NB * len(streams)
+        at = 8 * s + NB * streams[0]
+        yb, ps = T.yb[:, 48 * streams[0]:48 * i + 48], T["px%d" % i][:, 384:384 + nb]
         op("v", lambda: V.tensor_scalar(yb[:, 16:16 + 16 * nb], T.brw[:].indirect(T.offb[:, at:at + nb]), float(-HALF), None, A.add),
-           ["brw"] + obk, ["yb%d" % i], gcost(16 * nb), AT["yb"])
+           ["brw", "ybz"] + ["offb%d_%d_%d" % (s, x, b) for x in streams for b in range(NB)], ["yb%d" % i], gcost(16 * nb), AT["yb"])
 
         def turn():
             last = None
             for odd in (1, 0):
                 for b in range(nb):
                     for a in range(4):
-                        col = 2 * (2 * a + odd) + w
+                        n = 2 * (2 * a + odd) + w
                         last = PE.matmul(ps[32 * a:32 * a + 16 + 16 * odd, b:b + 1], yb[:, 16 * b + 16 - 16 * odd:16 * b + 32],
-                                         T.idn[:, col:col + 1], True, True)
+                                         T.idn[:, n:n + 1], True, True)
             return last
-        pe(turn, ["yb%d" % i, "ybz%d" % i, "idn"], ["B%d" % i], nb * 4 * 48, AT["bt"], "x%d" % i)
-        vec(lambda: V.tensor_scalar(T.snd[:, at:at + nb], ps, float(HALF), None, A.add), ["B%d" % i], ["snd%d_%d" % (s, i)], nb,
-            AT["snd"], bank="x%d" % i)
+        pe(turn, ["yb%d" % i, "idn"], ["B%d" % i], nb * 4 * 48, AT["bt"], "x%d" % i)
+        vec(lambda: V.tensor_scalar(T.snd[:, at:at + nb], ps, float(HALF), None, A.add), ["B%d" % i],
+            ["snd%d_%d" % (s, x) for x in streams], nb, AT["snd"], bank="x%d" % i)
 
-    def term(s, w, u, streams, bank):
-        i = streams[0]
-        nb = sum(WID[x] for x in streams)
-        n, j0, at = 16 * nb, 16 * B0[i], 16 * s + POS[i]
-        ps = T[bank][:, j0:j0 + n]
-        kk = "k%d" % w
-        win = T[kk][:].indirect(T.offb[:, at:at + nb])
-        ob = ["offb%d_%d_%d" % (s, x, b) for x in streams for b in range(WID[x])]
-        ks = lambda y: ["%s%d" % (y, x) for x in streams]
-        early = AT["yb"] - AT["kq"] if s == N - 1 else 0
-        op("v", lambda: V.tensor_tensor(T.kq[:, j0:j0 + n], win, T.qs[:, u * Q + j0:u * Q + j0 + n], A.mult),
-           [kk, "q%d" % u] + ob, ks("kq"), gcost(n), AT["kq"] + early)
-        pe(lambda: PE.matmul(ps, T.bo[:], T.kq[:, j0:j0 + n], True, True), ["bo"] + ks("kq"), ks("sb"), max(64, n), AT["sb"] + early, bank)
-        op("s", lambda: SC.activation(T.rs[:, j0:j0 + n], ps, F.Relu), ks("sb"), ks("rs"), vcost(n), AT["rs"] + early, bank=bank)
-        op("v", lambda: V.tensor_tensor(T.term[:, s * Q + j0:s * Q + j0 + n], win, T.rs[:, j0:j0 + n], A.mult), [kk] + ob + ks("rs"),
-           ks("term%d_" % s), gcost(n), AT["term"] + early)
+    def term(s, w, u, streams, bank, fast=True):
+        n, j0, at = 16 * NB * len(streams), 16 * NB * streams[0], 8 * s + NB * streams[0]
+        ps, out = T[bank][:, j0:j0 + n], T.term[:, s * Q + j0:s * Q + j0 + n]
+        kk = ["k%d" % w, "kz"] + ["offb%d_%d_%d" % (s, x, b) for x in streams for b in range(NB)]
+        win = T["k%d" % w][:].indirect(T.offb[:, at:at + NB * len(streams)])
+        ks = lambda y: ["%s%d_%d" % (y, s if y == "term" else s % 2, x) for x in streams]
+        at = (lambda x: AT["end"]) if s == N - 1 else (lambda x: AT[x])
+        kq, kb = (x[:, s % 2 * Q + j0:s % 2 * Q + j0 + n] for x in (T.kq, T.kb))
+        op("s", lambda: SC.activation(kb, win, F.Copy), kk, ks("kb"), 15.0 + gcost(n), at("kb"))
+        if fast:
+            op("v", lambda: V.tensor_tensor(kq, win, T.qs[:, u * Q + j0:u * Q + j0 + n], A.mult), kk + ["q%d" % u], ks("kq"), gcost(n), at("kq"))
+        else:
+            vec(lambda: V.tensor_tensor(kq, T.pq[:, u * Q + j0:u * Q + j0 + n], kb, A.mult), ks("kb") + ["pq%d" % u], ks("kq"), n, at("kq"), "q")
+        pe(lambda: PE.matmul(ps, T.bo[:], kq, True, True), ["bo"] + ks("kq"), ks("sb"), max(64, n), at("sb"), bank)
+        if s < N - 1:
+            op("s", lambda: SC.activation(ps, ps, F.Relu), ks("sb"), ks("sb"), vcost(n), at("rs"), bank=bank)
+        vec(lambda: V.tensor_tensor(out, ps, kb, A.mult), ks("sb") + ks("kb"), ks("term"), n, at("term"), bank)
 
     every = list(range(NS))
     part = lambda x, j0=0, n=Q: T[x[0]][:, x[1] * Q + j0:x[1] * Q + j0 + n]
     keys = lambda parts, streams: ["%s%d_%d" % (buf, t, i) for buf, t in parts for i in streams]
-    held, waiting, base = [], [], 0.0
+    held, kept, base = [], [], 0.0
     blocks(0, 0.0)
     for s in range(N):
         o = owner[s]
@@ -276,61 +248,62 @@ def build_ops(g, T, topo, r, P):
         came = s > 0 and walk[o][s - 1] != r
         now[0] = base
         if came:
-            held = [("pin", s)]
-            if u and owner[s - 1] == r:
-                blocks(1, AT["blocks"])
-        if s == N - 1 and len(held) > 1 and not FOLD:
+            held = [("pin", s)] * (s > 1) + (kept if o == r else [])
+            if u:
+                blocks(1, AT["blocks"], gathers[-1] if GATE else None)
+        if s == N - 1:
             vec(lambda held=held: V.tensor_tensor(T.acc[:], part(held[0]), part(held[1]), A.add), keys(held, every),
                 keys([("acc", 0)], every), 2 * Q, AT["acc"])
             held = [("acc", 0)]
         for i in every:
-            now[0] = base + AT["step"] * B0[i] / 8
-            nb, at = WID[i], 16 * s + POS[i]
+            now[0] = base + AT["step"] * i / NS
+            at = 8 * s + NB * i
             if s == 0:
-                src, srck = T.off0[:, at:at + nb], "off0_%d" % i
+                src, srck = T.off0[:, at:at + NB], "off0"
             else:
-                src, srck = T["land" if came else "snd"][:, at - 16:at - 16 + nb], "%s%d_%d" % ("land" if came else "snd", s - 1, i)
-            mid = T.mid[:, POS[i]:POS[i] + nb]
-            midk = ["mid%d_%d" % (i, b) for b in range(nb)]
-            obk = ["offb%d_%d_%d" % (s, i, b) for b in range(nb)]
-            step(w, u, i, src, [srck], mid, midk)
+                src, srck = T["land" if came else "snd"][:, at - 8:at - 8 + NB], "%s%d_%d" % ("land" if came else "snd", s - 1, i)
+            mid = T.mid[:, NB * i:NB * i + NB]
+            midk = ["mid%d_%d" % (i, b) for b in range(NB)]
+            obk = ["offb%d_%d_%d" % (s, i, b) for b in range(NB)]
+            step("start" if s == 0 else "came" if came else "first", w, u, i, src, [srck], mid, midk)
             now[0] += AT["step"]
-            step(w, u, i, mid, midk, T.offb[:, at:at + nb], obk)
+            step("last" if s == N - 1 else "second", w, u, i, mid, midk, T.offb[:, at:at + NB], obk)
             if s < N - 1:
-                bridge(w, s, i, obk)
+                for group in (OVER if stays else SENDS):
+                    if group[-1] == i:
+                        bridge(w, s, group)
                 for group in SENDS:
                     if not stays and group[-1] == i:
-                        a, b = 16 * s + POS[group[0]], at + nb
+                        a, b = 8 * s + NB * group[0], at + NB
                         send(partner[r], T.land[:, a:b], [T.snd[:, a:b]], "rm%d_%d" % (s + 1, i), keys([("snd", s)], group),
                              keys([("land", s)], group), P["hop"], AT["snd"])
             for group in LAST:
                 if s == N - 1 and group[-1] == i:
                     term(s, w, u, group, ("pt", "pb")[LAST.index(group) % 2])
-                    j0, n = 16 * B0[group[0]], 16 * sum(WID[x] for x in group)
+                    j0, n = 16 * NB * group[0], 16 * NB * len(group)
                     both, fin, pin = held + [("term", s)], ("fin", 0), ("pin", 0)
-                    if o == r or not FOLD:
+                    if o == r or FOLD < 2:
                         vec(lambda j0=j0, n=n, both=both: V.tensor_tensor(part(fin, j0, n), part(both[0], j0, n), part(both[1], j0, n), A.add),
-                            keys(both, group), keys([fin], group), 2 * n, AT["add"] + AT["yb"] - AT["kq"])
+                            keys(both, group), keys([fin], group), 2 * n, AT["end"])
                         both = [fin]
                     if o != r:
                         send(o, part(pin, j0, n), [part(x, j0, n) for x in both], "rm%d_%d" % (N, i), keys(both, group),
-                             keys([pin], group), P["hop"], AT["add"])
+                             keys([pin], group), P["hop"], AT["add"], wide=n)
                     out = fin if o == r else pin
-                    dmas("y", [(T.y[:, j0:j0 + n], part(out, j0, n))], "st", keys([out], group), [], 2000.0, AT["add"])
+                    dma("y", T.y[:, j0:j0 + n], part(out, j0, n), "st", keys([out], group), [], 2000.0, AT["add"])
         if s == 0:
-            dmas("y", [(T.brw[1:128:16, :], T.nb1[:, S:])], "lb1", ["nb1"], ["brw"], 2500.0, AT["yb"])
+            dma("y", T.brw[1:128:16, :], T.brd[:], "lb1", ["brd"], ["brw"], 2500.0, AT["yb"])
         if s < N - 1:
-            waiting.append((s, w, u))
-            if not stays or s == N - 2:
-                for n, x in enumerate(reversed(waiting)):
-                    for streams in ([every] if EVEN else [[i] for i in every]):
-                        now[0] = base + AT["step"] * (1 + B0[streams[-1]] / 8) + (AT["late"] if stays else AT["old"] * n)
-                        term(*x, streams, "pt")
-                waiting = []
+            now[0] = base + AT["step"] * (2 - 1 / NS) + AT["late" if stays else "gap" if s < N - 2 else "soon"]
+            term(s, w, u, every, ("pt", "pb")[s % 2], FAST and s == N - 2 and not stays)
             held = held + [("term", s)]
-            if not stays:
-                send(partner[r], part(("pin", s + 1)), [part(x) for x in held], "rp%d" % (s + 1), keys(held, every),
-                     keys([("pin", s + 1)], every), P["hop"], AT["add"])
+            if not stays and len(held) == 1:
+                kept = held
+            elif not stays:
+                vec(lambda held=held: V.tensor_tensor(T.sum[:], part(held[0]), part(held[1]), A.add), keys(held, every), ["sum"], 2 * Q,
+                    AT["term"])
+                send(partner[r], part(("pin", s + 1)), [T.sum[:]], "rp%d" % (s + 1), ["sum"], keys([("pin", s + 1)], every),
+                     P["hop"], AT["add"], wide=Q)
         base += 2 * AT["step"] + AT["bridge"] + (0 if stays else AT["cross"])
     return ops
 
@@ -362,7 +335,7 @@ def find_deps(ops):
 def ready_at(ops, m, start, lat):
     o = ops[m]
     return max([start[p] if p == o["behind"] or (ops[p]["eng"] == o["eng"] and not o["deps"].get(p, True) and not ops[p]["tok"])
-                else start[p] + ops[p]["cost"] + lat for p in o["pre"]], default=0.0)
+                else start[p] + ops[p]["cost"] + lat[ops[p]["eng"] == o["eng"]] for p in o["pre"]], default=0.0)
 
 
 def schedule(ops, lat, look):
@@ -397,7 +370,7 @@ def rank_program(g, core, T, topo):
         return
     ops = build_ops(g, T, topo, r, TIMES)
     find_deps(ops)
-    order = schedule(ops, TIMES["lat"], AT["look"])
+    order = schedule(ops, (TIMES["lat"], TIMES["own"]), AT["look"])
     place = {j: n for n, j in enumerate(order)}
     queue = {"v": g.vector, "s": g.scalar, "t": g.tensor, "g": g, "y": g.sync}
     counter = {"v": "cv", "s": "cs", "t": "ct", "g": "cg"}

import math
from concourse.bass import DstId, RemoteDMATransfer
from concourse.mybir import AluOpType as A, ActivationFunctionType as F, AxisListType as AX

N, S, Q = 4, 2304, 128
HALF = S // 2
BIG, GAIN = 21248.0, 1200.0
NONE = -1600.0
NS, NB = 4, 2
SHARE = dict(start=[14, 16, 10, 8], came=[10, 10, 12, 8], first=[2, 8, 12, 10], second=[8, 8, 8, 8], last=[6, 2, 6, 4])
SPLIT = dict(start=0, came=6, first=0, second=0, last=0)
SENDS = [[0], [1], [2], [3]]
LAST = [[0], [1], [2], [3]]
GATE = True
FAST = True
OVER = [[0], [1], [2], [3]]
FOLD = 0
AT = dict(c=-1440, cp=140, nodes=560, s=-60, v=520, xs=1510, turn=1380, scan=2200, fin=2340, yb=2780, bt=3120, snd=3140,
          kb=3140, kq=2740, sb=2680, rs=2980, term=3600, add=3740, acc=720, blocks=-780, step=2800, bridge=560, cross=1060,
          late=1880, gap=0, soon=120, end=2620, look=40)

SCRATCH = {_k: ("psum", [128, 512], "float32") for _k in ("pb", "pt", "pq")}
for _d, _bufs in (("int32", dict(nb0=S, nb1=S, brw=S, brc=S // 16, brd=S // 16, ent=8)),
                  ("bfloat16", dict(k0=S + 16, k1=S + 16, qs=2 * Q, qd0=8 * Q, qd1=8 * Q, bo=128, kq=2 * Q, kb=2 * Q,
                                    one=256, dup=256, sgn=68, sel=68, idn=16)),
                  ("uint16", dict(off0=8, mid=8, offb=8 * N, snd=8 * N, land=8 * N)),
                  ("float16", dict(yb=48 * NS)),
                  ("float32", dict(val=8, ta=8, tb=8, mg=8, col=8, gain=68, term=N * Q, pin=N * Q, sum=Q, acc=Q, fin=Q))):
    for _k, _n in _bufs.items():
        SCRATCH[_k] = ("sbuf", [128, _n], _d)
for _i in range(NS):
    for _k, _n, _d in (("c", 16 * NB, "uint16"), ("cp", 16 * NB, "float16"),
                       ("gk", 256 * NB, "bfloat16"), ("xs", 128, "float16"), ("r1", 68, "float32")):
        SCRATCH["%s%d" % (_k, _i)] = ("sbuf", [128, _n], _d)
    SCRATCH["px%d" % _i] = ("psum", [128, 512], "float32")

SEMAPHORES = (["cv", "cs", "ct", "cg", "le", "lq", "lnb", "lk", "lbr", "lbc", "lb1", "rnb", "rk", "rbr", "rq", "loc", "st"]
              + ["rp%d" % s for s in range(1, N)] + ["rm%d_%d" % (s, i) for s in range(1, N + 1) for i in range(NS)])

TIMES = dict(cy=0.9, ga=1.4, pe=0.4, pefix=170.0, lat=160.0, own=145.0, hop=1500.0, issue=400.0, column=14.0, load=4500.0, copy=9000.0)


def walkers(T, topo):
    near = [[t for t in range(N) if T.cores[t] in topo.cores_of(T.cores[o])] for o in range(N)]
    partner = [[t for t in range(N) if t not in near[o]][near[o].index(o)] for o in range(N)]
    return [[o if (o + s) % N in near[o] else partner[o] for s in range(N)] for o in range(N)], near, partner


def build_ops(g, T, topo, r, P):
    ops, gathers = [], []
    now = [-1.0e5]
    V, SC, PE, SY = g.vector, g.scalar, g.tensor, g.sync
    me = T.cores[r]
    walk, near, partner = walkers(T, topo)
    owner = [[o for o in range(N) if walk[o][s] == r][0] for s in range(N)]
    mate = [t for t in near[r] if t != r][0]
    vcost = lambda n: max(64.0, n) * P["cy"]
    gcost = lambda n: 60.0 * P["cy"] + P["ga"] * n
    engines = lambda a, b: len(topo.engines(T.cores[a], T.cores[b]))

    def op(eng, fn, rd, wr, cost, at=0.0, bank=None, hold=None, tok=None, after=None, loc=0, behind=None):
        ops.append(dict(eng=eng, fn=fn, rd=rd, wr=wr, cost=cost, bank=bank, hold=cost if hold is None else hold,
                        tok=tok, after=after, loc=loc, at=now[0] + at + 0.001 * len(ops), behind=behind))
        return len(ops) - 1

    def vec(fn, rd, wr, n, at=0.0, bank=None):
        op("v", fn, rd, wr, vcost(n), at, bank=bank)

    def pe(fn, rd, wr, cycles, at, bank):
        op("t", fn, rd, wr, P["pefix"] + cycles * P["pe"], at, bank=bank, hold=cycles * P["pe"])

    def dma(eng, out, in_, sem, rd, wr, cost, at=0.0, behind=None):
        q = {"y": SY, "s": SC}[eng]
        return op(eng, lambda: q.dma_start(out, in_).then_inc(T.sem[sem], 16), rd, wr, cost, at, hold=60.0, tok=(sem, 16), behind=behind)

    def send(to, dst, srcs, sem, rd, wr, time, at=0.0, issue=None, behind=None, wide=0):
        rid, pid = topo.addr(T.cores[to], me)
        mask = topo.mask(me, T.cores[to])
        if len(srcs) == 1:
            fn = lambda: g.remote_dma(dst, srcs[0], T.sem[sem], T.sem.loc, pid, rid, mask)
        else:
            fn = lambda: g.remote_dma_fused([RemoteDMATransfer(
                dst_ids=[DstId(rid=rid, pnc=pid)], dma_engine_mask=mask, remote_sem=T.sem[sem],
                srcs=srcs, dsts=[dst], alu_op=1)], local_sem=T.sem.loc)
        sent = op("g", fn, rd, [], issue or P["issue"], at, loc=engines(r, to), behind=behind)
        time += P["column"] * wide * len(srcs)
        op(None, None, [], wr, time, tok=(sem, engines(to, r)), after=sent)
        return sent

    a = dma("y", T.qs[:, 0:Q], T.q[:], "lq", [], ["q0"], 1800.0)
    a = dma("y", T.nb0[:], T.nb[:], "lnb", [], ["nb0"], P["load"] - 1200.0, behind=a)
    a = dma("y", T.k0[:, 0:S], T.k[:], "lk", [], ["k0"], P["load"], behind=a)
    a = dma("y", T.brc[:], T.br[:], "lbc", [], ["brc"], P["load"] + 200.0, behind=a)
    dma("s", T.ent[:], T.entry[:], "le", [], ["ent"], 1800.0)
    vec(lambda: V.memset(T.one[:], 1.0), [], ["one"], 128)
    vec(lambda: V.memset(T.k0[:, S:], 0.0), [], ["kz"], 16)
    for n in range(S // 256):
        vec(lambda n=n: V.memset(T.brw[:, 256 * n:256 * n + 256], 0), [], ["brz%d" % n], 256, 3.0)
    dma("y", T.brw[0:128:16, :], T.br[:], "lbr", ["brz%d" % n for n in range(S // 256)], ["brw"], 2500.0, behind=a)
    def pick(out, in_, pattern, base, test, fill, rd, wr, behind, sign=1):
        return op("g", lambda: g.affine_select(out, in_, [[sign * a, n] for a, n in pattern], test, fill, sign * base, -sign), rd, wr,
                  170.0 + 1.8 * math.prod(n for a, n in pattern), behind=behind)

    flag = dict(allow_small_or_imprecise_dtypes=True)
    a = op("g", lambda: g.iota(T.val[:], [[16, 8]], 0, -1, **flag), [], ["val"], 150.0)
    a = op("g", lambda: g.iota(T.sgn[:], [[0, NB], [-2, 2], [0, 17]], 1, 0, **flag), [], ["sgn"], 250.0, behind=a)
    a = pick(T.dup[:], T.one[:], [[16, 8], [0, 2], [1, 16]], 0, A.is_equal, 0.0, ["one"], ["dup"], a)
    a = pick(T.sgn[:], T.sgn[:], [[32, NB], [16, 2], [1, 17]], 64, A.is_equal, 0.0, ["sgn"], ["sgn"], a)
    a = pick(T.sel[:], T.sgn[:], [[32, NB], [0, 2], [1, 17]], 0, A.not_equal, BIG, ["sgn"], ["sel"], a)
    a = send(partner[r], T.qs[:, Q:2 * Q], [T.qs[:, 0:Q]], "rq", ["q0"], ["q1"], 4000.0, issue=2500.0, behind=a)
    a = send(mate, T.nb1[:], [T.nb0[:]], "rnb", ["nb0"], ["nb1"], P["copy"] - P["load"], behind=a)
    a = send(mate, T.k1[:], [T.k0[:]], "rk", ["k0", "kz"], ["k1"], P["copy"] - P["load"] - 500.0, behind=a)
    a = send(mate, T.brd[:], [T.brc[:]], "rbr", ["brc"], ["brd"], P["copy"] - P["load"] - 500.0, behind=a)
    a = pick(T.idn[:], T.one[:, 0:16], [[16, 8], [1, 2]], 0, A.is_equal, 0.0, ["one"], ["idn"], a)
    a = pick(T.bo[:], T.one[:, 0:128], [[16, 8], [0, 16]], 15, A.is_ge, 0.0, ["one"], ["bo"], a)
    pick(T.bo[:], T.bo[:], [[16, 8], [0, 16]], 0, A.is_ge, 0.0, ["bo"], ["bo"], a, -1)

    col, mg = (lambda n: T.col[:, n:n + 1]), (lambda n: T.mg[:, n:n + 1])
    vec(lambda: V.tensor_scalar(T.ta[:], T.val[:], -15.0, None, A.is_ge), ["val"], ["ta"], 8)
    vec(lambda: V.tensor_scalar(T.tb[:], T.val[:], 0.0, None, A.is_le), ["val"], ["tb"], 8)
    vec(lambda: V.memset(T.gain[:], GAIN), [], ["gain"], 68)
    vec(lambda: V.tensor_tensor(T.mg[:], T.ta[:], T.tb[:], A.mult), ["ta", "tb"], ["mg"], 16)
    vec(lambda: V.memset(T.gain[:, 0:68:17], -4.0e7), ["gain"], ["gain"], 4)
    vec(lambda: V.memset(T.yb[:], 0.0), [], ["ybz"], 96)
    vec(lambda: V.memset(T.gain[:, 16:68:17], 0.0), ["gain"], ["gain"], 4)
    ends = ((1.0, (5, 7)), (-1.0, (4, 6)))
    for n, (sign, rows) in enumerate(ends):
        vec(lambda n=n, sign=sign: V.tensor_scalar(col(4 + n), mg(1), 1.0 + sign * 2000.0, -sign * 2000.0, A.mult, A.add), ["mg"],
            ["col%d" % (4 + n)], 1)
    for m in range(2):
        for n, (sign, rows) in enumerate(ends):
            a, b = 4 - 2 * m + n, 2 - 2 * m + n
            vec(lambda a=a, b=b, sign=sign, row=rows[m]: V.tensor_scalar(col(b), mg(row), sign * 2000.0, col(a), A.mult, A.add),
                ["mg", "col%d" % a], ["col%d" % b], 1)
    for v in range(2):
        vec(lambda v=v: V.tensor_scalar(T.sel[:, 16 + 17 * v:68:34], T.one[:, 0:2], mg(1), (NONE - HALF * v) / 16, A.mult, A.mult),
            ["mg", "sel", "one"], ["sel%d" % v], 2)
    vec(lambda: V.tensor_copy(T.off0[:], T.ent[:]), ["ent"], ["off0"], 8)
    for i in range(NS):
        op("s", lambda i=i: SC.activation(T["px%d" % i][:, 0:128], T.one[:, 0:128], F.Copy, scale=0.0), ["one"], ["X%d" % i], vcost(128),
           bank="x%d" % i)

    def blocks(u, at, behind=None):
        for j in range(8):
            op("s", lambda j=j: SC.activation(T["qd%d" % u][:, Q * j:Q * j + Q], T.qs[:, u * Q:u * Q + Q], F.Copy, scale=T.mg[:, j:j + 1]),
               ["q%d" % u, "mg"], ["qd%d_%d" % (u, j)], vcost(Q), at, behind=behind)
        op("s", lambda: SC.activation(T.pq[:, u * Q:u * Q + Q], T.qs[:, u * Q:u * Q + Q], F.Copy), ["q%d" % u], ["pq%d" % u], vcost(Q),
           at, bank="q", behind=behind)

    def step(kind, w, u, i, src, srck, dst, dstk):
        n, read = 16 * NB, 16 if kind == "last" else 15
        c, cp, gk, xs, r1, px = (T["%s%d" % (x, i)] for x in ("c", "cp", "gk", "xs", "r1", "px"))
        qdk, nbk, kk = ["qd%d_%d" % (u, j) for j in range(8)], "nb%d" % w, "k%d" % w
        qd, pv = T["qd%d" % u], px[:, 128:196]
        k = lambda x: "%s%d" % (x, i)
        op("v", lambda: V.tensor_copy(c[:], T[nbk][:].indirect(src)), [nbk] + srck, [k("c")], gcost(n), AT["c"])
        vec(lambda: V.tensor_scalar(cp[:], c[:], float(-HALF), None, A.add), [k("c")], [k("cp")], n / 2, AT["cp"])
        xk = []
        for b in range(NB):
            def nodes(b=b):
                last = None
                for j in range(8):
                    last = PE.matmul(px[64 + 32 * b:96 + 32 * b, 16 * j:16 * j + 16], T.dup[:, 32 * j:32 * j + 32],
                                     cp[:, 16 * b:16 * b + 16], True, True)
                return last
            xk.append("D%d_%d" % (i, b))
            pe(nodes, [k("cp"), "dup", k("X")], [xk[-1]], 256, AT["nodes"], k("x"))
        j0 = 0
        due = {"v": AT["v"], "s": AT["s"]}
        mine, end = SHARE[kind][i], min(SPLIT[kind], max(0, n - SHARE[kind][i] - 8))
        for ci, (e, m) in enumerate((("s", n - mine - end), ("v", mine), ("s", end))):
            if not m:
                continue
            gkey = "g%d_%d" % (i, ci)
            o, win = gk[:, 16 * j0:16 * (j0 + m)], T[kk][:, 0:S].indirect(c[:, j0:j0 + m])
            if e == "v":
                op("v", lambda o=o, win=win: V.tensor_copy(o, win), [kk, k("c")], [gkey], gcost(16 * m), due[e])
            else:
                gathers.append(op("s", lambda o=o, win=win: SC.activation(o, win, F.Copy), [kk, k("c")], [gkey], 15.0 + gcost(16 * m), due[e]))
            due[e] += gcost(16 * m)

            def scores(j0=j0, m=m):
                last = None
                for j in range(j0, j0 + m):
                    b, a = j // 16, j % 16
                    last = PE.matmul(px[32 * b:32 * b + 16, a:128:16], gk[:, 16 * j:16 * j + 16],
                                     qd[:, n * i + j:8 * Q:Q], True, True)
                return last
            xk.append("X%d_%d" % (i, ci))
            pe(scores, [gkey, k("X")] + qdk, [xk[-1]], 16 * m, due[e] + P["lat"], k("x"))
            j0 += m
        vec(lambda: V.tensor_scalar(xs[:], px[:, 0:128], col(0), col(1), A.max, A.min), xk + ["col0", "col1"],
            [k("xs")], 128, AT["xs"], bank=k("x"))
        pe(lambda: PE.matmul(pv, xs[:], T.sel[:], True, True), [k("xs"), "sel0", "sel1"], [k("V")], 68, AT["turn"], k("x"))
        vec(lambda: V.tensor_tensor_scan(r1[:], T.gain[:], pv, 0.0, A.add, A.max), ["gain", k("V")], [k("r1")], 68, AT["scan"], bank=k("x"))
        for b in range(NB):
            e1, e2 = 34 * b + read, 34 * b + 17 + read
            vec(lambda b=b, e1=e1, e2=e2: V.tensor_scalar(dst[:, b:b + 1], r1[:, e1:e1 + 1], r1[:, e2:e2 + 1], float(HALF), A.subtract, A.add),
                [k("r1")], [dstk[b]], 1, AT["fin"])

    def bridge(w, s, streams):
        i, nb = streams[-1], NB * len(streams)
        at = 8 * s + NB * streams[0]
        yb, ps = T.yb[:, 48 * streams[0]:48 * i + 48], T["px%d" % i][:, 384:384 + nb]
        op("v", lambda: V.tensor_scalar(yb[:, 16:16 + 16 * nb], T.brw[:].indirect(T.offb[:, at:at + nb]), float(-HALF), None, A.add),
           ["brw", "ybz"] + ["offb%d_%d_%d" % (s, x, b) for x in streams for b in range(NB)], ["yb%d" % i], gcost(16 * nb), AT["yb"])

        def turn():
            last = None
            for odd in (1, 0):
                for b in range(nb):
                    for a in range(4):
                        n = 2 * (2 * a + odd) + w
                        last = PE.matmul(ps[32 * a:32 * a + 16 + 16 * odd, b:b + 1], yb[:, 16 * b + 16 - 16 * odd:16 * b + 32],
                                         T.idn[:, n:n + 1], True, True)
            return last
        pe(turn, ["yb%d" % i, "idn"], ["B%d" % i], nb * 4 * 48, AT["bt"], "x%d" % i)
        vec(lambda: V.tensor_scalar(T.snd[:, at:at + nb], ps, float(HALF), None, A.add), ["B%d" % i],
            ["snd%d_%d" % (s, x) for x in streams], nb, AT["snd"], bank="x%d" % i)

    def term(s, w, u, streams, bank, fast=True):
        n, j0, at = 16 * NB * len(streams), 16 * NB * streams[0], 8 * s + NB * streams[0]
        ps, out = T[bank][:, j0:j0 + n], T.term[:, s * Q + j0:s * Q + j0 + n]
        kk = ["k%d" % w, "kz"] + ["offb%d_%d_%d" % (s, x, b) for x in streams for b in range(NB)]
        win = T["k%d" % w][:].indirect(T.offb[:, at:at + NB * len(streams)])
        ks = lambda y: ["%s%d_%d" % (y, s if y == "term" else s % 2, x) for x in streams]
        at = (lambda x: AT["end"]) if s == N - 1 else (lambda x: AT[x])
        kq, kb = (x[:, s % 2 * Q + j0:s % 2 * Q + j0 + n] for x in (T.kq, T.kb))
        op("s", lambda: SC.activation(kb, win, F.Copy), kk, ks("kb"), 15.0 + gcost(n), at("kb"))
        if fast:
            op("v", lambda: V.tensor_tensor(kq, win, T.qs[:, u * Q + j0:u * Q + j0 + n], A.mult), kk + ["q%d" % u], ks("kq"), gcost(n), at("kq"))
        else:
            vec(lambda: V.tensor_tensor(kq, T.pq[:, u * Q + j0:u * Q + j0 + n], kb, A.mult), ks("kb") + ["pq%d" % u], ks("kq"), n, at("kq"), "q")
        pe(lambda: PE.matmul(ps, T.bo[:], kq, True, True), ["bo"] + ks("kq"), ks("sb"), max(64, n), at("sb"), bank)
        if s < N - 1:
            op("s", lambda: SC.activation(ps, ps, F.Relu), ks("sb"), ks("sb"), vcost(n), at("rs"), bank=bank)
        vec(lambda: V.tensor_tensor(out, ps, kb, A.mult), ks("sb") + ks("kb"), ks("term"), n, at("term"), bank)

    every = list(range(NS))
    part = lambda x, j0=0, n=Q: T[x[0]][:, x[1] * Q + j0:x[1] * Q + j0 + n]
    keys = lambda parts, streams: ["%s%d_%d" % (buf, t, i) for buf, t in parts for i in streams]
    held, kept, base = [], [], 0.0
    blocks(0, 0.0)
    for s in range(N):
        o = owner[s]
        u, w = 0 if o == r else 1, 0 if (o + s) % N == r else 1
        stays = s < N - 1 and walk[o][s + 1] == r
        came = s > 0 and walk[o][s - 1] != r
        now[0] = base
        if came:
            held = [("pin", s)] * (s > 1) + (kept if o == r else [])
            if u:
                blocks(1, AT["blocks"], gathers[-1] if GATE else None)
        if s == N - 1:
            vec(lambda held=held: V.tensor_tensor(T.acc[:], part(held[0]), part(held[1]), A.add), keys(held, every),
                keys([("acc", 0)], every), 2 * Q, AT["acc"])
            held = [("acc", 0)]
        for i in every:
            now[0] = base + AT["step"] * i / NS
            at = 8 * s + NB * i
            if s == 0:
                src, srck = T.off0[:, at:at + NB], "off0"
            else:
                src, srck = T["land" if came else "snd"][:, at - 8:at - 8 + NB], "%s%d_%d" % ("land" if came else "snd", s - 1, i)
            mid = T.mid[:, NB * i:NB * i + NB]
            midk = ["mid%d_%d" % (i, b) for b in range(NB)]
            obk = ["offb%d_%d_%d" % (s, i, b) for b in range(NB)]
            step("start" if s == 0 else "came" if came else "first", w, u, i, src, [srck], mid, midk)
            now[0] += AT["step"]
            step("last" if s == N - 1 else "second", w, u, i, mid, midk, T.offb[:, at:at + NB], obk)
            if s < N - 1:
                for group in (OVER if stays else SENDS):
                    if group[-1] == i:
                        bridge(w, s, group)
                for group in SENDS:
                    if not stays and group[-1] == i:
                        a, b = 8 * s + NB * group[0], at + NB
                        send(partner[r], T.land[:, a:b], [T.snd[:, a:b]], "rm%d_%d" % (s + 1, i), keys([("snd", s)], group),
                             keys([("land", s)], group), P["hop"], AT["snd"])
            for group in LAST:
                if s == N - 1 and group[-1] == i:
                    term(s, w, u, group, ("pt", "pb")[LAST.index(group) % 2])
                    j0, n = 16 * NB * group[0], 16 * NB * len(group)
                    both, fin, pin = held + [("term", s)], ("fin", 0), ("pin", 0)
                    if o == r or FOLD < 2:
                        vec(lambda j0=j0, n=n, both=both: V.tensor_tensor(part(fin, j0, n), part(both[0], j0, n), part(both[1], j0, n), A.add),
                            keys(both, group), keys([fin], group), 2 * n, AT["end"])
                        both = [fin]
                    if o != r:
                        send(o, part(pin, j0, n), [part(x, j0, n) for x in both], "rm%d_%d" % (N, i), keys(both, group),
                             keys([pin], group), P["hop"], AT["add"], wide=n)
                    out = fin if o == r else pin
                    dma("y", T.y[:, j0:j0 + n], part(out, j0, n), "st", keys([out], group), [], 2000.0, AT["add"])
        if s == 0:
            dma("y", T.brw[1:128:16, :], T.brd[:], "lb1", ["brd"], ["brw"], 2500.0, AT["yb"])
        if s < N - 1:
            now[0] = base + AT["step"] * (2 - 1 / NS) + AT["late" if stays else "gap" if s < N - 2 else "soon"]
            term(s, w, u, every, ("pt", "pb")[s % 2], FAST and s == N - 2 and not stays)
            held = held + [("term", s)]
            if not stays and len(held) == 1:
                kept = held
            elif not stays:
                vec(lambda held=held: V.tensor_tensor(T.sum[:], part(held[0]), part(held[1]), A.add), keys(held, every), ["sum"], 2 * Q,
                    AT["term"])
                send(partner[r], part(("pin", s + 1)), [T.sum[:]], "rp%d" % (s + 1), ["sum"], keys([("pin", s + 1)], every),
                     P["hop"], AT["add"], wide=Q)
        base += 2 * AT["step"] + AT["bridge"] + (0 if stays else AT["cross"])
    return ops


def find_deps(ops):
    writer, readers, banks = {}, {}, {}
    for n, o in enumerate(ops):
        d = {}
        for k in o["rd"]:
            if k in writer:
                d[writer[k]] = True
        for k in o["wr"]:
            for m in readers.get(k, []) + ([writer[k]] if k in writer else []):
                d.setdefault(m, False)
        if o["bank"] is not None:
            for e, m in banks.setdefault(o["bank"], {}).items():
                if e != o["eng"]:
                    d.setdefault(m, False)
            banks[o["bank"]][o["eng"]] = n
        for k in o["rd"]:
            readers.setdefault(k, []).append(n)
        for k in o["wr"]:
            writer[k], readers[k] = n, []
        d.pop(n, None)
        o["deps"] = d
        o["pre"] = list(d) + [m for m in (o["after"], o["behind"]) if m is not None]


def ready_at(ops, m, start, lat):
    o = ops[m]
    return max([start[p] if p == o["behind"] or (ops[p]["eng"] == o["eng"] and not o["deps"].get(p, True) and not ops[p]["tok"])
                else start[p] + ops[p]["cost"] + lat[ops[p]["eng"] == o["eng"]] for p in o["pre"]], default=0.0)


def schedule(ops, lat, look):
    n = len(ops)
    succ = [[] for _ in ops]
    for j in range(n):
        for m in ops[j]["pre"]:
            succ[m].append(j)
    left = [len(o["pre"]) for o in ops]
    ready = {j: 0.0 for j in range(n) if not left[j]}
    free, begin, order = {}, [0.0] * n, []
    while ready:
        start = {j: max(t, free.get(ops[j]["eng"], 0.0)) if ops[j]["eng"] else t for j, t in ready.items()}
        j = min(start, key=lambda x: (start[x], ops[x]["at"]))
        e = ops[j]["eng"]
        if e:
            j = min((x for x in start if ops[x]["eng"] == e and start[x] <= start[j] + look), key=lambda x: ops[x]["at"])
            free[e] = start[j] + ops[j]["hold"]
        begin[j] = start[j]
        order.append(j)
        del ready[j]
        for m in succ[j]:
            left[m] -= 1
            if not left[m]:
                ready[m] = ready_at(ops, m, begin, lat)
    return order


def rank_program(g, core, T, topo):
    r = T.rank_of(core)
    if r is None:
        return
    ops = build_ops(g, T, topo, r, TIMES)
    find_deps(ops)
    order = schedule(ops, (TIMES["lat"], TIMES["own"]), AT["look"])
    place = {j: n for n, j in enumerate(order)}
    queue = {"v": g.vector, "s": g.scalar, "t": g.tensor, "g": g, "y": g.sync}
    counter = {"v": "cv", "s": "cs", "t": "ct", "g": "cg"}
    known = {e: {} for e in queue}
    total, waited = {}, {}
    for j in order:
        o = ops[j]
        e = o["eng"]
        if e is None:
            o["done"], o["clock"] = o["tok"], {}
            total[o["tok"][0]] = o["tok"][1]
            continue
        for m in sorted(o["deps"], key=lambda x: -place[x]):
            p = ops[m]
            if p["eng"] == e and not o["deps"][m] and not p["tok"]:
                continue
            sem, val = p["done"]
            if known[e].get(sem, 0) < val:
                queue[e].wait_ge(T.sem[sem], val)
                waited[sem] = max(waited.get(sem, 0), val)
                known[e][sem] = val
                for x, v in p["clock"].items():
                    known[e][x] = max(known[e].get(x, 0), v)
        inst = o["fn"]()
        o["clock"] = dict(known[e])
        if o["loc"]:
            total["loc"] = total.get("loc", 0) + o["loc"]
            o["done"] = None
        elif o["tok"]:
            total[o["tok"][0]] = total.get(o["tok"][0], 0) + o["tok"][1]
            o["done"] = (o["tok"][0], total[o["tok"][0]])
        else:
            sem = counter[e]
            inst.then_inc(T.sem[sem], 1)
            total[sem] = total.get(sem, 0) + 1
            o["done"] = (sem, total[sem])
    for sem, val in total.items():
        if waited.get(sem, 0) < val:
            (g.sync if sem == "st" else g).wait_ge(T.sem[sem], val)
